import numpy as np
import ml_dtypes


def mxq(x, axis, fmt="e4m3"):
    dtype, down = {"e4m3": (ml_dtypes.float8_e4m3fn, 7), "e5m2": (ml_dtypes.float8_e5m2, 14)}[fmt]
    v = np.moveaxis(np.asarray(x, np.float32).astype(ml_dtypes.bfloat16).astype(np.float64), axis, -1)
    blocks = v.reshape(v.shape[:-1] + (-1, 32))
    amax = np.abs(blocks).max(-1, keepdims=True)
    byte = np.maximum(np.where(amax > 0, np.frexp(amax)[1] - 1 + 127, 0) - down, 1)
    scale = np.exp2(byte - 127.0)
    codes = (blocks / scale).astype(np.float32).astype(dtype).astype(np.float64)
    return np.moveaxis((codes * scale).reshape(v.shape), -1, axis)


WIDE = False


def mx_kscale(k):
    if not WIDE:
        return np.ones(k)
    levels = np.array([10, -10, 5, -5, 0])
    if k % 512:
        return np.exp2(np.random.permutation(np.resize(levels, k // 32))).repeat(32)
    a = np.empty((k // 512, 16))
    for p in range(k // 512):
        a[p, :8] = np.random.permutation(np.resize(levels, 8))
        for g in range(8):
            far = levels[np.abs(levels - a[p, g]) >= 10]
            a[p, g + 8] = far[np.random.randint(len(far))]
    return np.exp2(a.ravel()).repeat(32)


def f64(x):
    return np.asarray(x).astype(np.float64)


def striped(idx):
    return np.tile(idx.reshape(-1, 16).T, (8, 1)).astype(np.uint16)


def unstriped(offs):
    return offs[:16].T.reshape(-1).astype(np.int64)


def silu(v):
    return v / (1.0 + np.exp(-np.maximum(v, -700.0)))


K, T, S, H, N, U = 512, 2048, 1024, 512, 128, 1024


def setup_inputs():
    n = np.random.standard_normal
    s = mx_kscale(K)[:, None]
    u = mx_kscale(H)
    return {
        "xT": (n((K, T)) * s).astype(np.float32),
        "w1": (n((K, H)) / np.sqrt(2 * K) / s * u).astype(np.float32),
        "w2": (n((K, H)) / np.sqrt(2 * K) / s * u).astype(np.float32),
        "w3": (n((H, N)) / np.sqrt(H) / u[:, None]).astype(np.float32),
        "offs": striped(np.random.permutation(T)[:S]),
        "src": striped(np.random.permutation(S)[(S * np.random.uniform(0, 1, U) ** 4).astype(np.int64)]),
        "dst": striped(np.random.permutation(S)),
    }


def reference(xT, w1, w2, w3, offs, src, dst):
    xq = mxq(f64(xT)[:, unstriped(offs)], 0, "e4m3")
    y = mxq(f64(w1), 0, "e4m3").T @ xq
    e = mxq(f64(w2), 0, "e4m3").T @ xq
    z = silu(y[:, unstriped(src)] + e[:, unstriped(dst)])
    return mxq(f64(w3), 0, "e4m3").T @ mxq(z, 0, "e4m3")

@@ -1,0 +1,187 @@
+from contextlib import ExitStack
+
+import concourse.mybir as mybir
+
+K, T, S, H, N, U = 512, 2048, 1024, 512, 128, 1024
+FLOPS = 2 * K * H * S * 2 + 2 * H * N * U
+
+F32 = mybir.dt.float32
+BF16 = mybir.dt.bfloat16
+U32 = mybir.dt.uint32
+U16 = mybir.dt.uint16
+U8 = mybir.dt.uint8
+FP8X4 = mybir.dt.float8_e4m3fn_x4
+ADD = mybir.AluOpType.add
+SILU = mybir.ActivationFunctionType.Silu
+
+P = 128
+PACK = 4
+LIST_ROWS = 16
+
+NODE_PIECES = [(0, 256), (256, 512), (512, 768), (768, 1024)]
+FIRST_CUTS = [(0, 512), (512, 768), (768, 1024)]
+HALVES = [(0, 512), (512, 1024)]
+EDGE_PIECES = [(0, 512), (512, 768), (768, 896), (896, 1024)]
+
+
+def tile_picked_hub_silu_e_kernel(tc, xT, w1, w2, w3, offs, src, dst, out):
+    nc = tc.nc
+    with ExitStack() as ctx:
+        keep = ctx.enter_context(tc.tile_pool(name="keep", bufs=1))
+        psum = ctx.enter_context(tc.psum_pool(name="psum", bufs=6))
+        psum_out = ctx.enter_context(tc.psum_pool(name="psum_out", bufs=2))
+
+        offs_t = keep.tile([P, S // LIST_ROWS], U16, name="offs_t")
+        src_t = keep.tile([P, U // LIST_ROWS], U16, name="src_t")
+        dst_t = keep.tile([P, U // LIST_ROWS], U16, name="dst_t")
+
+        def entries(list_tile, a, b):
+            return list_tile[:, a // LIST_ROWS : b // LIST_ROWS]
+
+        warm = keep.tile([P, 1], F32, name="warm")
+        warm_out = keep.tile([P, 1], F32, name="warm_out")
+        nc.vector.memset(warm[:], 0.0)
+        nc.scalar.activation(warm_out[:], warm[:], SILU)
+
+        x_rows = xT.rearrange("(p u e) n -> u p e n", u=2, e=2)
+        chunks = [[(0, 1024), (1024, 2048)], [(0, 512), (512, 1024), (1024, 1536), (1536, 2048)]]
+        raw = {}
+        for u in range(2):
+            for a, b in chunks[u]:
+                raw[u, a] = keep.tile([P, 2, b - a], F32, name=f"raw_{u}_{a}")
+                nc.sync.dma_start(raw[u, a][:], x_rows[u][:, :, a:b])
+                if (u, a) == (0, 0):
+                    nc.sync.dma_start(offs_t[:], offs)
+        w_raw = []
+        for name, w in (("w1", w1), ("w2", w2)):
+            tile_w = keep.tile([P, PACK, H], F32, name=f"{name}_raw")
+            nc.sync.dma_start(tile_w[:], w.rearrange("(p j) c -> p j c", j=PACK))
+            w_raw.append(tile_w)
+            if name == "w1":
+                nc.sync.dma_start(src_t[:], src)
+        nc.sync.dma_start(dst_t[:], dst)
+        w3_raw = keep.tile([P, PACK, N], F32, name="w3_raw")
+        w3_rows = w3.rearrange("(b t q) n -> t b q n", t=PACK, q=8)
+        for t in range(PACK):
+            nc.sync.dma_start(w3_raw[:, t, :], w3_rows[t])
+
+        pairs = [keep.tile([P, T * 2], BF16, name=f"pairs_{u}", align_bytes=64) for u in range(2)]
+
+        def cast(engine_copy, u, a, lo, hi):
+            engine_copy(
+                pairs[u][:, 2 * (a + lo) : 2 * (a + hi)].rearrange("p (n e) -> p n e", e=2),
+                raw[u, a][:, :, lo:hi].rearrange("p e n -> p n e"),
+            )
+
+        picked = [keep.tile([P, 2, b - a], U32, name=f"picked_{a}") for a, b in NODE_PIECES]
+
+        def gather_nodes(u, i):
+            a, b = NODE_PIECES[i]
+            nc.vector.tensor_copy(picked[i][:, u, :], pairs[u][:].bitcast(U32).indirect(entries(offs_t, a, b)))
+
+        cast(nc.scalar.copy, 0, 0, 0, 1024)
+        cast(nc.vector.tensor_copy, 0, 1024, 0, 640)
+        cast(nc.scalar.copy, 0, 1024, 640, 1024)
+        for i in range(len(NODE_PIECES)):
+            gather_nodes(0, i)
+        cast(nc.scalar.copy, 1, 0, 0, 512)
+        cast(nc.scalar.copy, 1, 512, 0, 512)
+        cast(nc.vector.tensor_copy, 1, 1024, 0, 512)
+        cast(nc.vector.tensor_copy, 1, 1536, 0, 320)
+        cast(nc.scalar.copy, 1, 1536, 320, 512)
+
+        x_codes = keep.tile([P, S], U32, name="x_codes", align_bytes=64)
+        x_scales = keep.tile([P, S], U8, name="x_scales", align_bytes=64)
+        for i in range(len(NODE_PIECES)):
+            gather_nodes(1, i)
+        def weight_codes(side, t, engine_copy, tag):
+            grouped = keep.tile([P, P * PACK], BF16, name=f"wg_{side}_{t}", tag=tag, align_bytes=64)
+            engine_copy(
+                grouped[:].rearrange("p (b q j) -> p b q j", q=8, j=PACK),
+                w_raw[side][:].rearrange("p j (b t q) -> p t b q j", t=PACK, q=8)[:, t],
+            )
+            codes = keep.tile([P, P], U32, name=f"wc_{side}_{t}", align_bytes=64)
+            scales = keep.tile([P, P], U8, name=f"ws_{side}_{t}", align_bytes=64)
+            nc.vector.quantize_mx(out=codes[:].bitcast(FP8X4), scales=scales[:], in_=grouped[:])
+            return codes, scales
+
+        weights = {(0, 0): weight_codes(0, 0, nc.scalar.copy, "wg_0_0")}
+        for i, (a, b) in enumerate(NODE_PIECES):
+            woven = keep.tile([P, (b - a) * 2], U32, name=f"woven_{a}", tag=f"woven_{a}", align_bytes=64)
+            nc.scalar.copy(woven[:].rearrange("p (n u) -> p n u", u=2), picked[i][:].rearrange("p u n -> p n u"))
+            nc.vector.quantize_mx(out=x_codes[:, a:b].bitcast(FP8X4), scales=x_scales[:, a:b], in_=woven[:].bitcast(BF16))
+
+        def product(side, t, codes, scales, cuts):
+            result = keep.tile([P, S], F32, name=f"res_{side}_{t}")
+            for a, b in cuts:
+                acc = psum.tile([P, 512], F32, name="acc")
+                nc.tensor.matmul_mx(
+                    out=acc[:, : b - a],
+                    lhsT=codes[:].bitcast(FP8X4),
+                    lhsT_scale=scales[:],
+                    rhs=x_codes[:, a:b].bitcast(FP8X4),
+                    rhs_scale=x_scales[:, a:b],
+                    start=True,
+                    stop=True,
+                )
+                nc.scalar.copy(result[:, a:b], acc[:, : b - a])
+            return result
+
+        weights[0, 1] = weight_codes(0, 1, nc.vector.tensor_copy, "woven_768")
+        order = [(side, t) for side in range(2) for t in range(PACK)]
+        from_src = [keep.tile([P, PACK, 512], F32, name=f"from_src_{a}", tag=f"from_src_{a}", align_bytes=64) for a, b in HALVES]
+        res = {}
+        for n, (side, t) in enumerate(order):
+            if n >= 1:
+                for ahead in order[n + 1 : n + 3]:
+                    if ahead not in weights:
+                        weights[ahead] = weight_codes(ahead[0], ahead[1], nc.scalar.copy, f"wg_{ahead[0]}_{ahead[1]}")
+            codes, scales = weights[side, t]
+            res[side, t] = product(side, t, codes, scales, FIRST_CUTS if n == 0 else HALVES)
+            if side == 0:
+                for h, (a, b) in enumerate(HALVES):
+                    nc.vector.tensor_copy(from_src[h][:, t, :], res[0, t][:].indirect(entries(src_t, a, b)))
+
+        w3_grouped = keep.tile([P, N * PACK], BF16, name="w3_grouped", align_bytes=64)
+        nc.scalar.copy(w3_grouped[:].rearrange("p (n t) -> p n t", t=PACK), w3_raw[:].rearrange("p t n -> p n t"))
+        w3_codes = keep.tile([P, N], U32, name="w3_codes", align_bytes=64)
+        w3_scales = keep.tile([P, N], U8, name="w3_scales", align_bytes=64)
+        nc.vector.quantize_mx(out=w3_codes[:].bitcast(FP8X4), scales=w3_scales[:], in_=w3_grouped[:])
+
+        def finish(pre, a, b):
+            n = b - a
+            z = keep.tile([P, n * PACK], BF16, name=f"z_{a}", tag=f"z_{a}", align_bytes=64)
+            nc.scalar.activation(
+                z[:].rearrange("p (c i t) -> p c t i", i=4, t=PACK),
+                pre[:].rearrange("p t (c i) -> p c t i", i=4),
+                SILU,
+            )
+            z_codes = keep.tile([P, n], U32, name=f"zc_{a}", align_bytes=64)
+            z_scales = keep.tile([P, n], U8, name=f"zs_{a}", align_bytes=64)
+            nc.vector.quantize_mx(out=z_codes[:].bitcast(FP8X4), scales=z_scales[:], in_=z[:])
+            acc = psum_out.tile([P, 512], F32, name="acc_out")
+            nc.tensor.matmul_mx(
+                out=acc[:, :n],
+                lhsT=w3_codes[:].bitcast(FP8X4),
+                lhsT_scale=w3_scales[:],
+                rhs=z_codes[:].bitcast(FP8X4),
+                rhs_scale=z_scales[:],
+                start=True,
+                stop=True,
+            )
+            done = keep.tile([P, n], F32, name=f"done_{a}")
+            nc.scalar.copy(done[:], acc[:, :n])
+            nc.sync.dma_start(out[:, a:b], done[:])
+
+        pre_tags = ["pre_0", "from_src_0", "z_0", "z_512"]
+        for (a, b), tag in zip(EDGE_PIECES, pre_tags):
+            pre = keep.tile([P, PACK, b - a], F32, name=f"pre_{a}", tag=tag, align_bytes=64)
+            h = a // 512
+            for t in range(PACK):
+                nc.vector.tensor_tensor(
+                    pre[:, t, :],
+                    res[1, t][:].indirect(entries(dst_t, a, b)),
+                    from_src[h][:, t, a - 512 * h : b - 512 * h],
+                    ADD,
+                )
+            finish(pre, a, b)

@@ -1,6 +1,7 @@
 from contextlib import ExitStack
 
 import concourse.mybir as mybir
+from concourse.masks import make_identity
 
 K, T, S, H, N, U = 512, 2048, 1024, 512, 128, 1024
 FLOPS = 2 * K * H * S * 2 + 2 * H * N * U
@@ -19,17 +20,23 @@ PACK = 4
 LIST_ROWS = 16
 
 NODE_PIECES = [(0, 256), (256, 512), (512, 768), (768, 1024)]
-FIRST_CUTS = [(0, 512), (512, 768), (768, 1024)]
 HALVES = [(0, 512), (512, 1024)]
-EDGE_PIECES = [(0, 512), (512, 768), (768, 896), (896, 1024)]
+UNITS = [(0, 256), (256, 512), (512, 768)]
+TURNED = 768
+DIRECT = [(768, 896), (896, 1024)]
 
 
 def tile_picked_hub_silu_e_kernel(tc, xT, w1, w2, w3, offs, src, dst, out):
     nc = tc.nc
     with ExitStack() as ctx:
         keep = ctx.enter_context(tc.tile_pool(name="keep", bufs=1))
-        psum = ctx.enter_context(tc.psum_pool(name="psum", bufs=6))
-        psum_out = ctx.enter_context(tc.psum_pool(name="psum_out", bufs=2))
+        psum = ctx.enter_context(tc.psum_pool(name="psum", bufs=1))
+
+        def bank(n, name):
+            return psum.tile([P, 512], F32, name=name, tag=f"bank_{n}")
+
+        ident = keep.tile([P, P], F32, name="ident")
+        make_identity(nc, ident[:])
 
         offs_t = keep.tile([P, S // LIST_ROWS], U16, name="offs_t")
         src_t = keep.tile([P, U // LIST_ROWS], U16, name="src_t")
@@ -87,81 +94,142 @@ def tile_picked_hub_silu_e_kernel(tc, xT, w1, w2, w3, offs, src, dst, out):
         cast(nc.scalar.copy, 1, 0, 0, 512)
         cast(nc.scalar.copy, 1, 512, 0, 512)
         cast(nc.vector.tensor_copy, 1, 1024, 0, 512)
-        cast(nc.vector.tensor_copy, 1, 1536, 0, 320)
-        cast(nc.scalar.copy, 1, 1536, 320, 512)
+        cast(nc.vector.tensor_copy, 1, 1536, 0, 352)
+        cast(nc.scalar.copy, 1, 1536, 352, 512)
 
-        x_codes = keep.tile([P, S], U32, name="x_codes", align_bytes=64)
-        x_scales = keep.tile([P, S], U8, name="x_scales", align_bytes=64)
         for i in range(len(NODE_PIECES)):
             gather_nodes(1, i)
-        def weight_codes(side, t, engine_copy, tag):
-            grouped = keep.tile([P, P * PACK], BF16, name=f"wg_{side}_{t}", tag=tag, align_bytes=64)
-            engine_copy(
-                grouped[:].rearrange("p (b q j) -> p b q j", q=8, j=PACK),
-                w_raw[side][:].rearrange("p j (b t q) -> p t b q j", t=PACK, q=8)[:, t],
-            )
-            codes = keep.tile([P, P], U32, name=f"wc_{side}_{t}", align_bytes=64)
-            scales = keep.tile([P, P], U8, name=f"ws_{side}_{t}", align_bytes=64)
-            nc.vector.quantize_mx(out=codes[:].bitcast(FP8X4), scales=scales[:], in_=grouped[:])
-            return codes, scales
 
-        weights = {(0, 0): weight_codes(0, 0, nc.scalar.copy, "wg_0_0")}
+        weights = {}
+
+        def group_weights(side, t, engine_copy, grouped):
+            engine_copy(
+                grouped.rearrange("p (b g i j) -> p b g j i", g=2, i=4, j=PACK),
+                w_raw[side][:].rearrange("p j (b t g i) -> p t b g j i", t=PACK, g=2, i=4)[:, t],
+            )
+
+        def quantise_weights(tiles, grouped):
+            name = f"{tiles[0][0]}_{tiles[0][1]}"
+            codes = keep.tile([P, len(tiles) * P], U32, name=f"wc_{name}", align_bytes=64)
+            scales = keep.tile([P, len(tiles) * P], U8, name=f"ws_{name}", align_bytes=64)
+            nc.vector.quantize_mx(out=codes[:].bitcast(FP8X4), scales=scales[:], in_=grouped)
+            for n, key in enumerate(tiles):
+                weights[key] = (codes[:, n * P : (n + 1) * P], scales[:, n * P : (n + 1) * P])
+
+        first_grouped = keep.tile([P, 512], BF16, name="first_grouped", tag="x_codes_0", align_bytes=64)
+        group_weights(0, 0, nc.scalar.copy, first_grouped[:])
+        quantise_weights([(0, 0)], first_grouped[:])
+        x_codes = [keep.tile([P, 512], U32, name=f"x_codes_{a}", tag=f"x_codes_{a}", align_bytes=64) for a, b in HALVES]
+        x_scales = keep.tile([P, S], U8, name="x_scales", align_bytes=64)
+
+        def node_codes(a, b):
+            return x_codes[a // 512][:, a % 512 : a % 512 + b - a].bitcast(FP8X4)
+
         for i, (a, b) in enumerate(NODE_PIECES):
             woven = keep.tile([P, (b - a) * 2], U32, name=f"woven_{a}", tag=f"woven_{a}", align_bytes=64)
             nc.scalar.copy(woven[:].rearrange("p (n u) -> p n u", u=2), picked[i][:].rearrange("p u n -> p n u"))
-            nc.vector.quantize_mx(out=x_codes[:, a:b].bitcast(FP8X4), scales=x_scales[:, a:b], in_=woven[:].bitcast(BF16))
+            nc.vector.quantize_mx(out=node_codes(a, b), scales=x_scales[:, a:b], in_=woven[:].bitcast(BF16))
 
-        def product(side, t, codes, scales, cuts):
-            result = keep.tile([P, S], F32, name=f"res_{side}_{t}")
-            for a, b in cuts:
-                acc = psum.tile([P, 512], F32, name="acc")
+        def product(result, codes, scales, cuts, banks):
+            for (a, b), n in zip(cuts, banks):
+                acc = bank(n, "acc")
                 nc.tensor.matmul_mx(
                     out=acc[:, : b - a],
-                    lhsT=codes[:].bitcast(FP8X4),
-                    lhsT_scale=scales[:],
-                    rhs=x_codes[:, a:b].bitcast(FP8X4),
+                    lhsT=codes.bitcast(FP8X4),
+                    lhsT_scale=scales,
+                    rhs=node_codes(a, b),
                     rhs_scale=x_scales[:, a:b],
                     start=True,
                     stop=True,
                 )
                 nc.scalar.copy(result[:, a:b], acc[:, : b - a])
-            return result
 
-        weights[0, 1] = weight_codes(0, 1, nc.vector.tensor_copy, "woven_768")
+        grouped = keep.tile([P, 1024], BF16, name="grouped", tag="woven_768", align_bytes=64)
+        slots = [grouped[:, :512], grouped[:, 512:]]
+        group_weights(0, 1, nc.vector.tensor_copy, slots[0])
+        group_weights(0, 2, nc.vector.tensor_copy, slots[1])
+        quantise_weights([(0, 1), (0, 2)], grouped[:])
+        y = [keep.tile([P, S], F32, name=f"y_{t}") for t in range(PACK)]
+        e_low = [keep.tile([P, S], F32, name=f"e_{t}") for t in range(2)]
+        e_high = keep.tile([P, 2 * S], F32, name="e_high")
+        rows = {(0, t): y[t][:] for t in range(PACK)}
+        rows[1, 0] = e_low[0][:]
+        rows[1, 1] = e_low[1][:]
+        rows[1, 2] = e_high[:, :S]
+        rows[1, 3] = e_high[:, S:]
+        from_src = [keep.tile([P, TURNED], F32, name=f"from_src_{t}") for t in range(PACK)]
+        from_dst = {}
         order = [(side, t) for side in range(2) for t in range(PACK)]
-        from_src = [keep.tile([P, PACK, 512], F32, name=f"from_src_{a}", tag=f"from_src_{a}", align_bytes=64) for a, b in HALVES]
-        res = {}
         for n, (side, t) in enumerate(order):
-            if n >= 1:
-                for ahead in order[n + 1 : n + 3]:
-                    if ahead not in weights:
-                        weights[ahead] = weight_codes(ahead[0], ahead[1], nc.scalar.copy, f"wg_{ahead[0]}_{ahead[1]}")
+            if 1 <= n < len(order) - 2:
+                ahead = order[n + 2]
+                group_weights(ahead[0], ahead[1], nc.scalar.copy, slots[(n + 1) % 2])
+                quantise_weights([ahead], slots[(n + 1) % 2])
             codes, scales = weights[side, t]
-            res[side, t] = product(side, t, codes, scales, FIRST_CUTS if n == 0 else HALVES)
+            if n == 0:
+                product(rows[side, t], codes, scales, NODE_PIECES, [0, 1, 2, 3])
+            else:
+                product(rows[side, t], codes, scales, HALVES, [(2 * n - 2) % 4, (2 * n - 1) % 4])
             if side == 0:
-                for h, (a, b) in enumerate(HALVES):
-                    nc.vector.tensor_copy(from_src[h][:, t, :], res[0, t][:].indirect(entries(src_t, a, b)))
+                nc.vector.tensor_copy(from_src[t][:], y[t][:].indirect(entries(src_t, 0, TURNED)))
+            elif t < 2:
+                fetched = keep.tile([P, U], F32, name=f"from_dst_{t}")
+                for a, b in HALVES:
+                    nc.vector.tensor_copy(fetched[:, a:b], e_low[t][:].indirect(entries(dst_t, a, b)))
+                for a, b in UNITS + [(TURNED, U)]:
+                    from_dst[t, a] = fetched[:, a:b]
 
         w3_grouped = keep.tile([P, N * PACK], BF16, name="w3_grouped", align_bytes=64)
-        nc.scalar.copy(w3_grouped[:].rearrange("p (n t) -> p n t", t=PACK), w3_raw[:].rearrange("p t n -> p n t"))
+        nc.scalar.copy(
+            w3_grouped[:].rearrange("p (c i t) -> p c t i", i=4, t=PACK),
+            w3_raw[:].rearrange("p t (c i) -> p c t i", i=4),
+        )
         w3_codes = keep.tile([P, N], U32, name="w3_codes", align_bytes=64)
         w3_scales = keep.tile([P, N], U8, name="w3_scales", align_bytes=64)
         nc.vector.quantize_mx(out=w3_codes[:].bitcast(FP8X4), scales=w3_scales[:], in_=w3_grouped[:])
 
-        def finish(pre, a, b):
-            n = b - a
-            z = keep.tile([P, n * PACK], BF16, name=f"z_{a}", tag=f"z_{a}", align_bytes=64)
+        def fetch_high(a, b):
+            for t, window in ((2, e_high[:]), (3, e_high[:, S:])):
+                fetched = keep.tile([P, b - a], F32, name=f"from_dst_{t}_{a}")
+                nc.vector.tensor_copy(fetched[:], window.indirect(entries(dst_t, a, b)))
+                from_dst[t, a] = fetched[:]
+
+        def turned_sum(a, u, n, tag):
+            summed = bank(n, "summed")
+            steps = [(e, blk) for e in range(2) for blk in range(2)]
+            for k, (e, blk) in enumerate(steps):
+                nc.tensor.matmul(
+                    summed[:, (2 * blk + e) * P : (2 * blk + e + 1) * P],
+                    from_src[2 * u + e][:, a + blk * P : a + (blk + 1) * P],
+                    ident[:],
+                    is_transpose=True,
+                    start=(k == 0),
+                    stop=False,
+                )
+            for k, (e, blk) in enumerate(steps):
+                nc.tensor.matmul(
+                    summed[:, (2 * blk + e) * P : (2 * blk + e + 1) * P],
+                    from_dst[2 * u + e, a][:, blk * P : (blk + 1) * P],
+                    ident[:],
+                    is_transpose=True,
+                    start=False,
+                    stop=(k == len(steps) - 1),
+                )
+            turned = keep.tile([P, 512], BF16, name=f"turned_{a}_{u}", tag=tag, align_bytes=64)
             nc.scalar.activation(
-                z[:].rearrange("p (c i t) -> p c t i", i=4, t=PACK),
-                pre[:].rearrange("p t (c i) -> p c t i", i=4),
+                turned[:].rearrange("r (b p e) -> r b p e", b=2, e=2),
+                summed[:].rearrange("r (b e p) -> r b p e", b=2, e=2),
                 SILU,
             )
-            z_codes = keep.tile([P, n], U32, name=f"zc_{a}", align_bytes=64)
-            z_scales = keep.tile([P, n], U8, name=f"zs_{a}", align_bytes=64)
+            return turned
+
+        def second_product(z, a, b, n):
+            z_codes = keep.tile([P, b - a], U32, name=f"zc_{a}", align_bytes=64)
+            z_scales = keep.tile([P, b - a], U8, name=f"zs_{a}", align_bytes=64)
             nc.vector.quantize_mx(out=z_codes[:].bitcast(FP8X4), scales=z_scales[:], in_=z[:])
-            acc = psum_out.tile([P, 512], F32, name="acc_out")
+            acc = bank(n, "acc_out")
             nc.tensor.matmul_mx(
-                out=acc[:, :n],
+                out=acc[:, : b - a],
                 lhsT=w3_codes[:].bitcast(FP8X4),
                 lhsT_scale=w3_scales[:],
                 rhs=z_codes[:].bitcast(FP8X4),
@@ -169,19 +237,43 @@ def tile_picked_hub_silu_e_kernel(tc, xT, w1, w2, w3, offs, src, dst, out):
                 start=True,
                 stop=True,
             )
-            done = keep.tile([P, n], F32, name=f"done_{a}")
-            nc.scalar.copy(done[:], acc[:, :n])
+            done = keep.tile([P, b - a], F32, name=f"done_{a}")
+            nc.scalar.copy(done[:], acc[:, : b - a])
             nc.sync.dma_start(out[:, a:b], done[:])
 
-        pre_tags = ["pre_0", "from_src_0", "z_0", "z_512"]
-        for (a, b), tag in zip(EDGE_PIECES, pre_tags):
+        turned_low = [turned_sum(a, 0, [7, 0, 1][i], f"low_{i}") for i, (a, b) in enumerate(UNITS)]
+        for i, (a, b) in enumerate(UNITS):
+            fetch_high(a, b)
+            halves = [turned_low[i], turned_sum(a, 1, 4 + i, f"high_{i % 2}")]
+            back = bank([2, 3, 7][i], "back")
+            for blk in range(2):
+                for u in range(2):
+                    nc.tensor.transpose(
+                        back[:, (2 * blk + u) * P : (2 * blk + u + 1) * P],
+                        halves[u][:].bitcast(F32)[:, blk * P : (blk + 1) * P],
+                        ident[:],
+                    )
+            z = keep.tile([P, (b - a) * PACK], BF16, name=f"z_{a}", tag=f"z_{a}", align_bytes=64)
+            nc.scalar.copy(
+                z[:].bitcast(F32).rearrange("p (b r u) -> p b r u", b=2, u=2),
+                back[:].rearrange("p (b u r) -> p b r u", b=2, u=2),
+            )
+            second_product(z, a, b, 4 + i)
+
+        fetch_high(TURNED, U)
+        for i, ((a, b), tag) in enumerate(zip(DIRECT, ["z_0", "z_256"])):
             pre = keep.tile([P, PACK, b - a], F32, name=f"pre_{a}", tag=tag, align_bytes=64)
-            h = a // 512
             for t in range(PACK):
                 nc.vector.tensor_tensor(
                     pre[:, t, :],
-                    res[1, t][:].indirect(entries(dst_t, a, b)),
-                    from_src[h][:, t, a - 512 * h : b - 512 * h],
+                    y[t][:].indirect(entries(src_t, a, b)),
+                    from_dst[t, TURNED][:, a - TURNED : b - TURNED],
                     ADD,
                 )
-            finish(pre, a, b)
+            z = keep.tile([P, (b - a) * PACK], BF16, name=f"z_{a}", tag=f"high_{i}", align_bytes=64)
+            nc.scalar.activation(
+                z[:].rearrange("p (c i t) -> p c t i", i=4, t=PACK),
+                pre[:].rearrange("p t (c i) -> p c t i", i=4),
+                SILU,
+            )
+            second_product(z, a, b, i)

@@ -1,7 +1,6 @@
 from contextlib import ExitStack
 
 import concourse.mybir as mybir
-from concourse.masks import make_identity
 
 K, T, S, H, N, U = 512, 2048, 1024, 512, 128, 1024
 FLOPS = 2 * K * H * S * 2 + 2 * H * N * U
@@ -21,9 +20,7 @@ LIST_ROWS = 16
 
 NODE_PIECES = [(0, 256), (256, 512), (512, 768), (768, 1024)]
 HALVES = [(0, 512), (512, 1024)]
-UNITS = [(0, 256), (256, 512), (512, 768)]
-TURNED = 768
-DIRECT = [(768, 896), (896, 1024)]
+EDGE_PIECES = [(0, 512), (512, 768), (768, 896), (896, 1024)]
 
 
 def tile_picked_hub_silu_e_kernel(tc, xT, w1, w2, w3, offs, src, dst, out):
@@ -35,9 +32,6 @@ def tile_picked_hub_silu_e_kernel(tc, xT, w1, w2, w3, offs, src, dst, out):
         def bank(n, name):
             return psum.tile([P, 512], F32, name=name, tag=f"bank_{n}")
 
-        ident = keep.tile([P, P], F32, name="ident")
-        make_identity(nc, ident[:])
-
         offs_t = keep.tile([P, S // LIST_ROWS], U16, name="offs_t")
         src_t = keep.tile([P, U // LIST_ROWS], U16, name="src_t")
         dst_t = keep.tile([P, U // LIST_ROWS], U16, name="dst_t")
@@ -45,13 +39,8 @@ def tile_picked_hub_silu_e_kernel(tc, xT, w1, w2, w3, offs, src, dst, out):
         def entries(list_tile, a, b):
             return list_tile[:, a // LIST_ROWS : b // LIST_ROWS]
 
-        warm = keep.tile([P, 1], F32, name="warm")
-        warm_out = keep.tile([P, 1], F32, name="warm_out")
-        nc.vector.memset(warm[:], 0.0)
-        nc.scalar.activation(warm_out[:], warm[:], SILU)
-
         x_rows = xT.rearrange("(p u e) n -> u p e n", u=2, e=2)
-        chunks = [[(0, 1024), (1024, 2048)], [(0, 512), (512, 1024), (1024, 1536), (1536, 2048)]]
+        chunks = [[(0, 1024), (1024, 2048)], [(0, 1024), (1024, 1536), (1536, 2048)]]
         raw = {}
         for u in range(2):
             for a, b in chunks[u]:
@@ -91,8 +80,8 @@ def tile_picked_hub_silu_e_kernel(tc, xT, w1, w2, w3, offs, src, dst, out):
         cast(nc.scalar.copy, 0, 1024, 640, 1024)
         for i in range(len(NODE_PIECES)):
             gather_nodes(0, i)
-        cast(nc.scalar.copy, 1, 0, 0, 512)
-        cast(nc.scalar.copy, 1, 512, 0, 512)
+        cast(nc.scalar.copy, 1, 0, 0, 768)
+        cast(nc.vector.tensor_copy, 1, 0, 768, 1024)
         cast(nc.vector.tensor_copy, 1, 1024, 0, 512)
         cast(nc.vector.tensor_copy, 1, 1536, 0, 352)
         cast(nc.scalar.copy, 1, 1536, 352, 512)
@@ -149,16 +138,8 @@ def tile_picked_hub_silu_e_kernel(tc, xT, w1, w2, w3, offs, src, dst, out):
         group_weights(0, 1, nc.vector.tensor_copy, slots[0])
         group_weights(0, 2, nc.vector.tensor_copy, slots[1])
         quantise_weights([(0, 1), (0, 2)], grouped[:])
-        y = [keep.tile([P, S], F32, name=f"y_{t}") for t in range(PACK)]
-        e_low = [keep.tile([P, S], F32, name=f"e_{t}") for t in range(2)]
-        e_high = keep.tile([P, 2 * S], F32, name="e_high")
-        rows = {(0, t): y[t][:] for t in range(PACK)}
-        rows[1, 0] = e_low[0][:]
-        rows[1, 1] = e_low[1][:]
-        rows[1, 2] = e_high[:, :S]
-        rows[1, 3] = e_high[:, S:]
-        from_src = [keep.tile([P, TURNED], F32, name=f"from_src_{t}") for t in range(PACK)]
-        from_dst = {}
+        rows = {(side, t): keep.tile([P, S], F32, name=f"rows_{side}_{t}") for side in range(2) for t in range(PACK)}
+        from_src = [keep.tile([P, PACK, 512], F32, name=f"from_src_{a}", tag=f"from_src_{a}", align_bytes=64) for a, b in HALVES]
         order = [(side, t) for side in range(2) for t in range(PACK)]
         for n, (side, t) in enumerate(order):
             if 1 <= n < len(order) - 2:
@@ -171,13 +152,8 @@ def tile_picked_hub_silu_e_kernel(tc, xT, w1, w2, w3, offs, src, dst, out):
             else:
                 product(rows[side, t], codes, scales, HALVES, [(2 * n - 2) % 4, (2 * n - 1) % 4])
             if side == 0:
-                nc.vector.tensor_copy(from_src[t][:], y[t][:].indirect(entries(src_t, 0, TURNED)))
-            elif t < 2:
-                fetched = keep.tile([P, U], F32, name=f"from_dst_{t}")
-                for a, b in HALVES:
-                    nc.vector.tensor_copy(fetched[:, a:b], e_low[t][:].indirect(entries(dst_t, a, b)))
-                for a, b in UNITS + [(TURNED, U)]:
-                    from_dst[t, a] = fetched[:, a:b]
+                for h, (a, b) in enumerate(HALVES):
+                    nc.vector.tensor_copy(from_src[h][:, t, :], rows[0, t][:].indirect(entries(src_t, a, b)))
 
         w3_grouped = keep.tile([P, N * PACK], BF16, name="w3_grouped", align_bytes=64)
         nc.scalar.copy(
@@ -187,41 +163,6 @@ def tile_picked_hub_silu_e_kernel(tc, xT, w1, w2, w3, offs, src, dst, out):
         w3_codes = keep.tile([P, N], U32, name="w3_codes", align_bytes=64)
         w3_scales = keep.tile([P, N], U8, name="w3_scales", align_bytes=64)
         nc.vector.quantize_mx(out=w3_codes[:].bitcast(FP8X4), scales=w3_scales[:], in_=w3_grouped[:])
-
-        def fetch_high(a, b):
-            for t, window in ((2, e_high[:]), (3, e_high[:, S:])):
-                fetched = keep.tile([P, b - a], F32, name=f"from_dst_{t}_{a}")
-                nc.vector.tensor_copy(fetched[:], window.indirect(entries(dst_t, a, b)))
-                from_dst[t, a] = fetched[:]
-
-        def turned_sum(a, u, n, tag):
-            summed = bank(n, "summed")
-            steps = [(e, blk) for e in range(2) for blk in range(2)]
-            for k, (e, blk) in enumerate(steps):
-                nc.tensor.matmul(
-                    summed[:, (2 * blk + e) * P : (2 * blk + e + 1) * P],
-                    from_src[2 * u + e][:, a + blk * P : a + (blk + 1) * P],
-                    ident[:],
-                    is_transpose=True,
-                    start=(k == 0),
-                    stop=False,
-                )
-            for k, (e, blk) in enumerate(steps):
-                nc.tensor.matmul(
-                    summed[:, (2 * blk + e) * P : (2 * blk + e + 1) * P],
-                    from_dst[2 * u + e, a][:, blk * P : (blk + 1) * P],
-                    ident[:],
-                    is_transpose=True,
-                    start=False,
-                    stop=(k == len(steps) - 1),
-                )
-            turned = keep.tile([P, 512], BF16, name=f"turned_{a}_{u}", tag=tag, align_bytes=64)
-            nc.scalar.activation(
-                turned[:].rearrange("r (b p e) -> r b p e", b=2, e=2),
-                summed[:].rearrange("r (b e p) -> r b p e", b=2, e=2),
-                SILU,
-            )
-            return turned
 
         def second_product(z, a, b, n):
             z_codes = keep.tile([P, b - a], U32, name=f"zc_{a}", align_bytes=64)
@@ -241,39 +182,30 @@ def tile_picked_hub_silu_e_kernel(tc, xT, w1, w2, w3, offs, src, dst, out):
             nc.scalar.copy(done[:], acc[:, : b - a])
             nc.sync.dma_start(out[:, a:b], done[:])
 
-        turned_low = [turned_sum(a, 0, [7, 0, 1][i], f"low_{i}") for i, (a, b) in enumerate(UNITS)]
-        for i, (a, b) in enumerate(UNITS):
-            fetch_high(a, b)
-            halves = [turned_low[i], turned_sum(a, 1, 4 + i, f"high_{i % 2}")]
-            back = bank([2, 3, 7][i], "back")
-            for blk in range(2):
-                for u in range(2):
-                    nc.tensor.transpose(
-                        back[:, (2 * blk + u) * P : (2 * blk + u + 1) * P],
-                        halves[u][:].bitcast(F32)[:, blk * P : (blk + 1) * P],
-                        ident[:],
-                    )
-            z = keep.tile([P, (b - a) * PACK], BF16, name=f"z_{a}", tag=f"z_{a}", align_bytes=64)
-            nc.scalar.copy(
-                z[:].bitcast(F32).rearrange("p (b r u) -> p b r u", b=2, u=2),
-                back[:].rearrange("p (b u r) -> p b r u", b=2, u=2),
-            )
-            second_product(z, a, b, 4 + i)
-
-        fetch_high(TURNED, U)
-        for i, ((a, b), tag) in enumerate(zip(DIRECT, ["z_0", "z_256"])):
-            pre = keep.tile([P, PACK, b - a], F32, name=f"pre_{a}", tag=tag, align_bytes=64)
+        def edge_values(pre, a, b):
+            h = a // 512
             for t in range(PACK):
                 nc.vector.tensor_tensor(
                     pre[:, t, :],
-                    y[t][:].indirect(entries(src_t, a, b)),
-                    from_dst[t, TURNED][:, a - TURNED : b - TURNED],
+                    rows[1, t][:].indirect(entries(dst_t, a, b)),
+                    from_src[h][:, t, a - 512 * h : b - 512 * h],
                     ADD,
                 )
-            z = keep.tile([P, (b - a) * PACK], BF16, name=f"z_{a}", tag=f"high_{i}", align_bytes=64)
+            z = keep.tile([P, (b - a) * PACK], BF16, name=f"z_{a}", tag=f"z_{a}", align_bytes=64)
             nc.scalar.activation(
                 z[:].rearrange("p (c i t) -> p c t i", i=4, t=PACK),
-                pre[:].rearrange("p t (c i) -> p c t i", i=4),
+                pre.rearrange("p t (c i) -> p c t i", i=4),
                 SILU,
             )
-            second_product(z, a, b, i)
+            return z
+
+        pre_first = keep.tile([P, PACK, 512], F32, name="pre_first")
+        second_product(edge_values(pre_first[:], 0, 512), 0, 512, 4)
+        pre_mid = keep.tile([P, PACK * 384], F32, name="pre_mid", tag="from_src_0", align_bytes=64)
+        z_b = edge_values(pre_mid[:, :1024].rearrange("p (t n) -> p t n", t=PACK), 512, 768)
+        z_c = edge_values(pre_mid[:, 1024:].rearrange("p (t n) -> p t n", t=PACK), 768, 896)
+        pre_last = keep.tile([P, PACK, 128], F32, name="pre_last", tag="z_0", align_bytes=64)
+        z_d = edge_values(pre_last[:], 896, 1024)
+        second_product(z_b, 512, 768, 5)
+        second_product(z_c, 768, 896, 6)
+        second_product(z_d, 896, 1024, 7)

@@ -17,10 +17,18 @@ SILU = mybir.ActivationFunctionType.Silu
 P = 128
 PACK = 4
 LIST_ROWS = 16
+BANK = 512
+BLOCK_ROWS = 8
+RUN = 4
 
-NODE_PIECES = [(0, 256), (256, 512), (512, 768), (768, 1024)]
-HALVES = [(0, 512), (512, 1024)]
-EDGE_PIECES = [(0, 512), (512, 768), (768, 896), (896, 1024)]
+X_LOADS = [(0, 1024), (1024, 1536), (1536, 2048)]
+LAST_LOAD_VECTOR = 352
+WIDE_LOAD_SCALAR = 896
+
+NODE_QUARTERS = [(0, 256), (256, 512), (512, 768), (768, 1024)]
+HALVES = [(0, BANK), (BANK, 2 * BANK)]
+FIRST_BANKS = 4
+EDGES_A, EDGES_B, EDGES_C, EDGES_D = (0, 512), (512, 768), (768, 896), (896, 1024)
 
 
 def tile_picked_hub_silu_e_kernel(tc, xT, w1, w2, w3, offs, src, dst, out):
@@ -29,8 +37,8 @@ def tile_picked_hub_silu_e_kernel(tc, xT, w1, w2, w3, offs, src, dst, out):
         keep = ctx.enter_context(tc.tile_pool(name="keep", bufs=1))
         psum = ctx.enter_context(tc.psum_pool(name="psum", bufs=1))
 
-        def bank(n, name):
-            return psum.tile([P, 512], F32, name=name, tag=f"bank_{n}")
+        def bank(number, name):
+            return psum.tile([P, BANK], F32, name=name, tag=f"bank_{number}")
 
         offs_t = keep.tile([P, S // LIST_ROWS], U16, name="offs_t")
         src_t = keep.tile([P, U // LIST_ROWS], U16, name="src_t")
@@ -40,61 +48,54 @@ def tile_picked_hub_silu_e_kernel(tc, xT, w1, w2, w3, offs, src, dst, out):
             return list_tile[:, a // LIST_ROWS : b // LIST_ROWS]
 
         x_rows = xT.rearrange("(p u e) n -> u p e n", u=2, e=2)
-        chunks = [[(0, 1024), (1024, 2048)], [(0, 1024), (1024, 1536), (1536, 2048)]]
         raw = {}
         for u in range(2):
-            for a, b in chunks[u]:
+            for a, b in X_LOADS:
                 raw[u, a] = keep.tile([P, 2, b - a], F32, name=f"raw_{u}_{a}")
                 nc.sync.dma_start(raw[u, a][:], x_rows[u][:, :, a:b])
-                if (u, a) == (0, 0):
+                if len(raw) == 1:
                     nc.sync.dma_start(offs_t[:], offs)
         w_raw = []
-        for name, w in (("w1", w1), ("w2", w2)):
+        for name, w, list_tile, list_in in (("w1", w1, src_t, src), ("w2", w2, dst_t, dst)):
             tile_w = keep.tile([P, PACK, H], F32, name=f"{name}_raw")
             nc.sync.dma_start(tile_w[:], w.rearrange("(p j) c -> p j c", j=PACK))
             w_raw.append(tile_w)
-            if name == "w1":
-                nc.sync.dma_start(src_t[:], src)
-        nc.sync.dma_start(dst_t[:], dst)
+            nc.sync.dma_start(list_tile[:], list_in)
         w3_raw = keep.tile([P, PACK, N], F32, name="w3_raw")
-        w3_rows = w3.rearrange("(b t q) n -> t b q n", t=PACK, q=8)
+        w3_rows = w3.rearrange("(b t q) n -> t b q n", t=PACK, q=BLOCK_ROWS)
         for t in range(PACK):
             nc.sync.dma_start(w3_raw[:, t, :], w3_rows[t])
 
         pairs = [keep.tile([P, T * 2], BF16, name=f"pairs_{u}", align_bytes=64) for u in range(2)]
 
-        def cast(engine_copy, u, a, lo, hi):
+        def round_pairs(engine_copy, u, load, lo, hi):
+            a = load[0]
             engine_copy(
                 pairs[u][:, 2 * (a + lo) : 2 * (a + hi)].rearrange("p (n e) -> p n e", e=2),
                 raw[u, a][:, :, lo:hi].rearrange("p e n -> p n e"),
             )
 
-        picked = [keep.tile([P, 2, b - a], U32, name=f"picked_{a}") for a, b in NODE_PIECES]
-
-        def gather_nodes(u, i):
-            a, b = NODE_PIECES[i]
-            nc.vector.tensor_copy(picked[i][:, u, :], pairs[u][:].bitcast(U32).indirect(entries(offs_t, a, b)))
-
-        cast(nc.scalar.copy, 0, 0, 0, 1024)
-        cast(nc.vector.tensor_copy, 0, 1024, 0, 640)
-        cast(nc.scalar.copy, 0, 1024, 640, 1024)
-        for i in range(len(NODE_PIECES)):
-            gather_nodes(0, i)
-        cast(nc.scalar.copy, 1, 0, 0, 768)
-        cast(nc.vector.tensor_copy, 1, 0, 768, 1024)
-        cast(nc.vector.tensor_copy, 1, 1024, 0, 512)
-        cast(nc.vector.tensor_copy, 1, 1536, 0, 352)
-        cast(nc.scalar.copy, 1, 1536, 352, 512)
-
-        for i in range(len(NODE_PIECES)):
-            gather_nodes(1, i)
+        picked = [keep.tile([P, 2, b - a], U32, name=f"picked_{a}") for a, b in NODE_QUARTERS]
+        wide, middle, last = X_LOADS
+        for u in range(2):
+            wide_n, middle_n, last_n = [b - a for a, b in X_LOADS]
+            if u == 0:
+                round_pairs(nc.scalar.copy, u, wide, 0, wide_n)
+            else:
+                round_pairs(nc.scalar.copy, u, wide, 0, WIDE_LOAD_SCALAR)
+                round_pairs(nc.vector.tensor_copy, u, wide, WIDE_LOAD_SCALAR, wide_n)
+            round_pairs(nc.vector.tensor_copy, u, middle, 0, middle_n)
+            round_pairs(nc.vector.tensor_copy, u, last, 0, LAST_LOAD_VECTOR)
+            round_pairs(nc.scalar.copy, u, last, LAST_LOAD_VECTOR, last_n)
+            for quarter, (a, b) in zip(picked, NODE_QUARTERS):
+                nc.vector.tensor_copy(quarter[:, u, :], pairs[u][:].bitcast(U32).indirect(entries(offs_t, a, b)))
 
         weights = {}
 
         def group_weights(side, t, engine_copy, grouped):
             engine_copy(
-                grouped.rearrange("p (b g i j) -> p b g j i", g=2, i=4, j=PACK),
-                w_raw[side][:].rearrange("p j (b t g i) -> p t b g j i", t=PACK, g=2, i=4)[:, t],
+                grouped.rearrange("p (b g i j) -> p b g j i", g=BLOCK_ROWS // RUN, i=RUN, j=PACK),
+                w_raw[side][:].rearrange("p j (b t g i) -> p t b g j i", t=PACK, g=BLOCK_ROWS // RUN, i=RUN)[:, t],
             )
 
         def quantise_weights(tiles, grouped):
@@ -105,70 +106,71 @@ def tile_picked_hub_silu_e_kernel(tc, xT, w1, w2, w3, offs, src, dst, out):
             for n, key in enumerate(tiles):
                 weights[key] = (codes[:, n * P : (n + 1) * P], scales[:, n * P : (n + 1) * P])
 
-        first_grouped = keep.tile([P, 512], BF16, name="first_grouped", tag="x_codes_0", align_bytes=64)
+        first_grouped = keep.tile([P, P * PACK], BF16, name="first_grouped", align_bytes=64)
         group_weights(0, 0, nc.scalar.copy, first_grouped[:])
         quantise_weights([(0, 0)], first_grouped[:])
-        x_codes = [keep.tile([P, 512], U32, name=f"x_codes_{a}", tag=f"x_codes_{a}", align_bytes=64) for a, b in HALVES]
+
+        x_codes = keep.tile([P, S], U32, name="x_codes", align_bytes=64)
         x_scales = keep.tile([P, S], U8, name="x_scales", align_bytes=64)
-
-        def node_codes(a, b):
-            return x_codes[a // 512][:, a % 512 : a % 512 + b - a].bitcast(FP8X4)
-
-        for i, (a, b) in enumerate(NODE_PIECES):
+        for quarter, (a, b) in zip(picked, NODE_QUARTERS):
             woven = keep.tile([P, (b - a) * 2], U32, name=f"woven_{a}", tag=f"woven_{a}", align_bytes=64)
-            nc.scalar.copy(woven[:].rearrange("p (n u) -> p n u", u=2), picked[i][:].rearrange("p u n -> p n u"))
-            nc.vector.quantize_mx(out=node_codes(a, b), scales=x_scales[:, a:b], in_=woven[:].bitcast(BF16))
+            nc.scalar.copy(woven[:].rearrange("p (n u) -> p n u", u=2), quarter[:].rearrange("p u n -> p n u"))
+            nc.vector.quantize_mx(out=x_codes[:, a:b].bitcast(FP8X4), scales=x_scales[:, a:b], in_=woven[:].bitcast(BF16))
 
-        def product(result, codes, scales, cuts, banks):
-            for (a, b), n in zip(cuts, banks):
-                acc = bank(n, "acc")
+        def first_product(result, codes, scales, cuts, banks):
+            for (a, b), number in zip(cuts, banks):
+                acc = bank(number, "acc")
                 nc.tensor.matmul_mx(
                     out=acc[:, : b - a],
                     lhsT=codes.bitcast(FP8X4),
                     lhsT_scale=scales,
-                    rhs=node_codes(a, b),
+                    rhs=x_codes[:, a:b].bitcast(FP8X4),
                     rhs_scale=x_scales[:, a:b],
                     start=True,
                     stop=True,
                 )
                 nc.scalar.copy(result[:, a:b], acc[:, : b - a])
 
-        grouped = keep.tile([P, 1024], BF16, name="grouped", tag="woven_768", align_bytes=64)
-        slots = [grouped[:, :512], grouped[:, 512:]]
+        last_woven = f"woven_{NODE_QUARTERS[-1][0]}"
+        grouped = keep.tile([P, 2 * P * PACK], BF16, name="grouped", tag=last_woven, align_bytes=64)
+        slots = [grouped[:, : P * PACK], grouped[:, P * PACK :]]
         group_weights(0, 1, nc.vector.tensor_copy, slots[0])
         group_weights(0, 2, nc.vector.tensor_copy, slots[1])
         quantise_weights([(0, 1), (0, 2)], grouped[:])
+
         rows = {(side, t): keep.tile([P, S], F32, name=f"rows_{side}_{t}") for side in range(2) for t in range(PACK)}
-        from_src = [keep.tile([P, PACK, 512], F32, name=f"from_src_{a}", tag=f"from_src_{a}", align_bytes=64) for a, b in HALVES]
+        from_src = [keep.tile([P, PACK, BANK], F32, name=f"from_src_{a}", tag=f"from_src_{a}", align_bytes=64) for a, b in HALVES]
         order = [(side, t) for side in range(2) for t in range(PACK)]
         for n, (side, t) in enumerate(order):
-            if 1 <= n < len(order) - 2:
+            if n + 2 < len(order) and order[n + 2] not in weights:
                 ahead = order[n + 2]
                 group_weights(ahead[0], ahead[1], nc.scalar.copy, slots[(n + 1) % 2])
                 quantise_weights([ahead], slots[(n + 1) % 2])
             codes, scales = weights[side, t]
             if n == 0:
-                product(rows[side, t], codes, scales, NODE_PIECES, [0, 1, 2, 3])
+                first_product(rows[side, t], codes, scales, NODE_QUARTERS, range(FIRST_BANKS))
             else:
-                product(rows[side, t], codes, scales, HALVES, [(2 * n - 2) % 4, (2 * n - 1) % 4])
+                banks = [(2 * n - 2) % FIRST_BANKS, (2 * n - 1) % FIRST_BANKS]
+                first_product(rows[side, t], codes, scales, HALVES, banks)
             if side == 0:
-                for h, (a, b) in enumerate(HALVES):
-                    nc.vector.tensor_copy(from_src[h][:, t, :], rows[0, t][:].indirect(entries(src_t, a, b)))
+                for half, (a, b) in zip(from_src, HALVES):
+                    nc.vector.tensor_copy(half[:, t, :], rows[0, t][:].indirect(entries(src_t, a, b)))
 
         w3_grouped = keep.tile([P, N * PACK], BF16, name="w3_grouped", align_bytes=64)
         nc.scalar.copy(
-            w3_grouped[:].rearrange("p (c i t) -> p c t i", i=4, t=PACK),
-            w3_raw[:].rearrange("p t (c i) -> p c t i", i=4),
+            w3_grouped[:].rearrange("p (c i t) -> p c t i", i=RUN, t=PACK),
+            w3_raw[:].rearrange("p t (c i) -> p c t i", i=RUN),
         )
         w3_codes = keep.tile([P, N], U32, name="w3_codes", align_bytes=64)
         w3_scales = keep.tile([P, N], U8, name="w3_scales", align_bytes=64)
         nc.vector.quantize_mx(out=w3_codes[:].bitcast(FP8X4), scales=w3_scales[:], in_=w3_grouped[:])
 
-        def second_product(z, a, b, n):
+        def second_product(z, edges, number):
+            a, b = edges
             z_codes = keep.tile([P, b - a], U32, name=f"zc_{a}", align_bytes=64)
             z_scales = keep.tile([P, b - a], U8, name=f"zs_{a}", align_bytes=64)
             nc.vector.quantize_mx(out=z_codes[:].bitcast(FP8X4), scales=z_scales[:], in_=z[:])
-            acc = bank(n, "acc_out")
+            acc = bank(number, "acc_out")
             nc.tensor.matmul_mx(
                 out=acc[:, : b - a],
                 lhsT=w3_codes[:].bitcast(FP8X4),
@@ -182,30 +184,34 @@ def tile_picked_hub_silu_e_kernel(tc, xT, w1, w2, w3, offs, src, dst, out):
             nc.scalar.copy(done[:], acc[:, : b - a])
             nc.sync.dma_start(out[:, a:b], done[:])
 
-        def edge_values(pre, a, b):
-            h = a // 512
+        def edge_values(sums, edges):
+            a, b = edges
+            half = a // BANK
             for t in range(PACK):
                 nc.vector.tensor_tensor(
-                    pre[:, t, :],
+                    sums[:, t, :],
                     rows[1, t][:].indirect(entries(dst_t, a, b)),
-                    from_src[h][:, t, a - 512 * h : b - 512 * h],
+                    from_src[half][:, t, a - BANK * half : b - BANK * half],
                     ADD,
                 )
             z = keep.tile([P, (b - a) * PACK], BF16, name=f"z_{a}", tag=f"z_{a}", align_bytes=64)
             nc.scalar.activation(
-                z[:].rearrange("p (c i t) -> p c t i", i=4, t=PACK),
-                pre.rearrange("p t (c i) -> p c t i", i=4),
+                z[:].rearrange("p (c i t) -> p c t i", i=RUN, t=PACK),
+                sums.rearrange("p t (c i) -> p c t i", i=RUN),
                 SILU,
             )
             return z
 
-        pre_first = keep.tile([P, PACK, 512], F32, name="pre_first")
-        second_product(edge_values(pre_first[:], 0, 512), 0, 512, 4)
-        pre_mid = keep.tile([P, PACK * 384], F32, name="pre_mid", tag="from_src_0", align_bytes=64)
-        z_b = edge_values(pre_mid[:, :1024].rearrange("p (t n) -> p t n", t=PACK), 512, 768)
-        z_c = edge_values(pre_mid[:, 1024:].rearrange("p (t n) -> p t n", t=PACK), 768, 896)
-        pre_last = keep.tile([P, PACK, 128], F32, name="pre_last", tag="z_0", align_bytes=64)
-        z_d = edge_values(pre_last[:], 896, 1024)
-        second_product(z_b, 512, 768, 5)
-        second_product(z_c, 768, 896, 6)
-        second_product(z_d, 896, 1024, 7)
+        def width(edges):
+            return edges[1] - edges[0]
+
+        sums_a = keep.tile([P, PACK, width(EDGES_A)], F32, name="pre_first")
+        second_product(edge_values(sums_a[:], EDGES_A), EDGES_A, FIRST_BANKS)
+        split = PACK * width(EDGES_B)
+        sums_bc = keep.tile([P, split + PACK * width(EDGES_C)], F32, name="pre_mid", tag="from_src_0", align_bytes=64)
+        z_b = edge_values(sums_bc[:, :split].rearrange("p (t n) -> p t n", t=PACK), EDGES_B)
+        z_c = edge_values(sums_bc[:, split:].rearrange("p (t n) -> p t n", t=PACK), EDGES_C)
+        sums_d = keep.tile([P, PACK, width(EDGES_D)], F32, name="pre_last", tag="z_0", align_bytes=64)
+        z_d = edge_values(sums_d[:], EDGES_D)
+        for n, (z, edges) in enumerate(((z_b, EDGES_B), (z_c, EDGES_C), (z_d, EDGES_D))):
+            second_product(z, edges, FIRST_BANKS + 1 + n)

@@ -21,9 +21,8 @@ BANK = 512
 BLOCK_ROWS = 8
 RUN = 4
 
-X_LOADS = [(0, 1024), (1024, 1536), (1536, 2048)]
-LAST_LOAD_VECTOR = 352
-WIDE_LOAD_SCALAR = 896
+X_CUTS = [(0, 896, 1664, 2048), (0, 768, 1536, 2048)]
+VECTOR_SIXTEENTHS = [(10, 10, 10), (6, 11, 11)]
 
 NODE_QUARTERS = [(0, 256), (256, 512), (512, 768), (768, 1024)]
 HALVES = [(0, BANK), (BANK, 2 * BANK)]
@@ -47,13 +46,13 @@ def tile_picked_hub_silu_e_kernel(tc, xT, w1, w2, w3, offs, src, dst, out):
         def entries(list_tile, a, b):
             return list_tile[:, a // LIST_ROWS : b // LIST_ROWS]
 
-        x_rows = xT.rearrange("(p u e) n -> u p e n", u=2, e=2)
-        raw = {}
+        x_rows = xT.rearrange("(p u e) n -> u p (e n)", u=2, e=2)
+        raw = [keep.tile([P, 2 * T], F32, name=f"raw_{u}") for u in range(2)]
         for u in range(2):
-            for a, b in X_LOADS:
-                raw[u, a] = keep.tile([P, 2, b - a], F32, name=f"raw_{u}_{a}")
-                nc.sync.dma_start(raw[u, a][:], x_rows[u][:, :, a:b])
-                if len(raw) == 1:
+            for a, b in zip(X_CUTS[u], X_CUTS[u][1:]):
+                start = T + a if a else 0
+                nc.sync.dma_start(raw[u][:, start : T + b], x_rows[u][:, start : T + b])
+                if u == 0 and a == 0:
                     nc.sync.dma_start(offs_t[:], offs)
         w_raw = []
         for name, w, list_tile, list_in in (("w1", w1, src_t, src), ("w2", w2, dst_t, dst)):
@@ -68,25 +67,18 @@ def tile_picked_hub_silu_e_kernel(tc, xT, w1, w2, w3, offs, src, dst, out):
 
         pairs = [keep.tile([P, T * 2], BF16, name=f"pairs_{u}", align_bytes=64) for u in range(2)]
 
-        def round_pairs(engine_copy, u, load, lo, hi):
-            a = load[0]
+        def round_pairs(engine_copy, u, lo, hi):
             engine_copy(
-                pairs[u][:, 2 * (a + lo) : 2 * (a + hi)].rearrange("p (n e) -> p n e", e=2),
-                raw[u, a][:, :, lo:hi].rearrange("p e n -> p n e"),
+                pairs[u][:, 2 * lo : 2 * hi].rearrange("p (n e) -> p n e", e=2),
+                raw[u][:].rearrange("p (e n) -> p n e", e=2)[:, lo:hi, :],
             )
 
         picked = [keep.tile([P, 2, b - a], U32, name=f"picked_{a}") for a, b in NODE_QUARTERS]
-        wide, middle, last = X_LOADS
         for u in range(2):
-            wide_n, middle_n, last_n = [b - a for a, b in X_LOADS]
-            if u == 0:
-                round_pairs(nc.scalar.copy, u, wide, 0, wide_n)
-            else:
-                round_pairs(nc.scalar.copy, u, wide, 0, WIDE_LOAD_SCALAR)
-                round_pairs(nc.vector.tensor_copy, u, wide, WIDE_LOAD_SCALAR, wide_n)
-            round_pairs(nc.vector.tensor_copy, u, middle, 0, middle_n)
-            round_pairs(nc.vector.tensor_copy, u, last, 0, LAST_LOAD_VECTOR)
-            round_pairs(nc.scalar.copy, u, last, LAST_LOAD_VECTOR, last_n)
+            for a, b, share in zip(X_CUTS[u], X_CUTS[u][1:], VECTOR_SIXTEENTHS[u]):
+                middle = a + (b - a) * share // 16
+                round_pairs(nc.vector.tensor_copy, u, a, middle)
+                round_pairs(nc.scalar.copy, u, middle, b)
             for quarter, (a, b) in zip(picked, NODE_QUARTERS):
                 nc.vector.tensor_copy(quarter[:, u, :], pairs[u][:].bitcast(U32).indirect(entries(offs_t, a, b)))
 

@@ -22,7 +22,7 @@ BLOCK_ROWS = 8
 RUN = 4
 
 X_CUTS = [(0, 896, 1664, 2048), (0, 768, 1536, 2048)]
-VECTOR_SIXTEENTHS = [(10, 10, 10), (6, 11, 11)]
+VECTOR_SIXTEENTHS = [(10, 10, 10), (9, 11, 11)]
 
 NODE_QUARTERS = [(0, 256), (256, 512), (512, 768), (768, 1024)]
 HALVES = [(0, BANK), (BANK, 2 * BANK)]
@@ -58,7 +58,7 @@ def tile_picked_hub_silu_e_kernel(tc, xT, w1, w2, w3, offs, src, dst, out):
         for name, w, list_tile, list_in in (("w1", w1, src_t, src), ("w2", w2, dst_t, dst)):
             tile_w = keep.tile([P, PACK, H], F32, name=f"{name}_raw")
             nc.sync.dma_start(tile_w[:], w.rearrange("(p j) c -> p j c", j=PACK))
-            w_raw.append(tile_w)
+            w_raw.append(tile_w[:])
             nc.sync.dma_start(list_tile[:], list_in)
         w3_raw = keep.tile([P, PACK, N], F32, name="w3_raw")
         w3_rows = w3.rearrange("(b t q) n -> t b q n", t=PACK, q=BLOCK_ROWS)
@@ -73,21 +73,22 @@ def tile_picked_hub_silu_e_kernel(tc, xT, w1, w2, w3, offs, src, dst, out):
                 raw[u][:].rearrange("p (e n) -> p n e", e=2)[:, lo:hi, :],
             )
 
-        picked = [keep.tile([P, 2, b - a], U32, name=f"picked_{a}") for a, b in NODE_QUARTERS]
+        picked_tile = keep.tile([P, 2 * S], U32, name="picked", align_bytes=64)
+        picked = picked_tile[:].rearrange("p (u n) -> p u n", u=2)
         for u in range(2):
             for a, b, share in zip(X_CUTS[u], X_CUTS[u][1:], VECTOR_SIXTEENTHS[u]):
                 middle = a + (b - a) * share // 16
                 round_pairs(nc.vector.tensor_copy, u, a, middle)
                 round_pairs(nc.scalar.copy, u, middle, b)
-            for quarter, (a, b) in zip(picked, NODE_QUARTERS):
-                nc.vector.tensor_copy(quarter[:, u, :], pairs[u][:].bitcast(U32).indirect(entries(offs_t, a, b)))
+            for a, b in NODE_QUARTERS if u else [(0, S)]:
+                nc.vector.tensor_copy(picked[:, u, a:b], pairs[u][:].bitcast(U32).indirect(entries(offs_t, a, b)))
 
         weights = {}
 
         def group_weights(side, t, engine_copy, grouped):
             engine_copy(
                 grouped.rearrange("p (b g i j) -> p b g j i", g=BLOCK_ROWS // RUN, i=RUN, j=PACK),
-                w_raw[side][:].rearrange("p j (b t g i) -> p t b g j i", t=PACK, g=BLOCK_ROWS // RUN, i=RUN)[:, t],
+                w_raw[side].rearrange("p j (b t g i) -> p t b g j i", t=PACK, g=BLOCK_ROWS // RUN, i=RUN)[:, t],
             )
 
         def quantise_weights(tiles, grouped):
@@ -104,10 +105,10 @@ def tile_picked_hub_silu_e_kernel(tc, xT, w1, w2, w3, offs, src, dst, out):
 
         x_codes = keep.tile([P, S], U32, name="x_codes", align_bytes=64)
         x_scales = keep.tile([P, S], U8, name="x_scales", align_bytes=64)
-        for quarter, (a, b) in zip(picked, NODE_QUARTERS):
-            woven = keep.tile([P, (b - a) * 2], U32, name=f"woven_{a}", tag=f"woven_{a}", align_bytes=64)
-            nc.scalar.copy(woven[:].rearrange("p (n u) -> p n u", u=2), quarter[:].rearrange("p u n -> p n u"))
-            nc.vector.quantize_mx(out=x_codes[:, a:b].bitcast(FP8X4), scales=x_scales[:, a:b], in_=woven[:].bitcast(BF16))
+        for a, b in NODE_QUARTERS:
+            woven = keep.tile([P, (b - a) * 2], U32, name=f"woven_{a}", align_bytes=64)[:]
+            nc.scalar.copy(woven.rearrange("p (n u) -> p n u", u=2), picked[:, :, a:b].rearrange("p u n -> p n u"))
+            nc.vector.quantize_mx(out=x_codes[:, a:b].bitcast(FP8X4), scales=x_scales[:, a:b], in_=woven.bitcast(BF16))
 
         def first_product(result, codes, scales, cuts, banks):
             for (a, b), number in zip(cuts, banks):
@@ -123,15 +124,16 @@ def tile_picked_hub_silu_e_kernel(tc, xT, w1, w2, w3, offs, src, dst, out):
                 )
                 nc.scalar.copy(result[:, a:b], acc[:, : b - a])
 
-        last_woven = f"woven_{NODE_QUARTERS[-1][0]}"
-        grouped = keep.tile([P, 2 * P * PACK], BF16, name="grouped", tag=last_woven, align_bytes=64)
-        slots = [grouped[:, : P * PACK], grouped[:, P * PACK :]]
+        slots = [picked[:, u, NODE_QUARTERS[-1][0] :].bitcast(BF16) for u in range(2)]
         group_weights(0, 1, nc.vector.tensor_copy, slots[0])
         group_weights(0, 2, nc.vector.tensor_copy, slots[1])
-        quantise_weights([(0, 1), (0, 2)], grouped[:])
+        quantise_weights([(0, 1)], slots[0])
+        quantise_weights([(0, 2)], slots[1])
 
         rows = {(side, t): keep.tile([P, S], F32, name=f"rows_{side}_{t}") for side in range(2) for t in range(PACK)}
-        from_src = [keep.tile([P, PACK, BANK], F32, name=f"from_src_{a}", tag=f"from_src_{a}", align_bytes=64) for a, b in HALVES]
+        src_low = keep.tile([P, (PACK + 1) * BANK], F32, name="src_low")
+        src_high = keep.tile([P, PACK * BANK], F32, name="src_high")
+        from_src = [half[:, : PACK * BANK].rearrange("p (t n) -> p t n", t=PACK) for half in (src_low, src_high)]
         order = [(side, t) for side in range(2) for t in range(PACK)]
         for n, (side, t) in enumerate(order):
             if n + 2 < len(order) and order[n + 2] not in weights:
@@ -157,11 +159,22 @@ def tile_picked_hub_silu_e_kernel(tc, xT, w1, w2, w3, offs, src, dst, out):
         w3_scales = keep.tile([P, N], U8, name="w3_scales", align_bytes=64)
         nc.vector.quantize_mx(out=w3_codes[:].bitcast(FP8X4), scales=w3_scales[:], in_=w3_grouped[:])
 
-        def second_product(z, edges, number):
+        def quantise_edges(z, edges, cuts):
             a, b = edges
             z_codes = keep.tile([P, b - a], U32, name=f"zc_{a}", align_bytes=64)
             z_scales = keep.tile([P, b - a], U8, name=f"zs_{a}", align_bytes=64)
-            nc.vector.quantize_mx(out=z_codes[:].bitcast(FP8X4), scales=z_scales[:], in_=z[:])
+            step = (b - a) // cuts
+            for lo in range(0, b - a, step):
+                nc.vector.quantize_mx(
+                    out=z_codes[:, lo : lo + step].bitcast(FP8X4),
+                    scales=z_scales[:, lo : lo + step],
+                    in_=z[:, PACK * lo : PACK * (lo + step)],
+                )
+            return z_codes, z_scales
+
+        def second_product(quantised, edges, number):
+            a, b = edges
+            z_codes, z_scales = quantised
             acc = bank(number, "acc_out")
             nc.tensor.matmul_mx(
                 out=acc[:, : b - a],
@@ -176,17 +189,17 @@ def tile_picked_hub_silu_e_kernel(tc, xT, w1, w2, w3, offs, src, dst, out):
             nc.scalar.copy(done[:], acc[:, : b - a])
             nc.sync.dma_start(out[:, a:b], done[:])
 
-        def edge_values(sums, edges):
+        def edge_values(sums, edges, tiles):
             a, b = edges
             half = a // BANK
-            for t in range(PACK):
+            for t in tiles:
                 nc.vector.tensor_tensor(
                     sums[:, t, :],
                     rows[1, t][:].indirect(entries(dst_t, a, b)),
                     from_src[half][:, t, a - BANK * half : b - BANK * half],
                     ADD,
                 )
-            z = keep.tile([P, (b - a) * PACK], BF16, name=f"z_{a}", tag=f"z_{a}", align_bytes=64)
+            z = keep.tile([P, (b - a) * PACK], BF16, name=f"z_{a}", align_bytes=64)
             nc.scalar.activation(
                 z[:].rearrange("p (c i t) -> p c t i", i=RUN, t=PACK),
                 sums.rearrange("p t (c i) -> p c t i", i=RUN),
@@ -197,13 +210,16 @@ def tile_picked_hub_silu_e_kernel(tc, xT, w1, w2, w3, offs, src, dst, out):
         def width(edges):
             return edges[1] - edges[0]
 
+        in_order = range(PACK)
+        last_first = [PACK - 1, *range(PACK - 1)]
         sums_a = keep.tile([P, PACK, width(EDGES_A)], F32, name="pre_first")
-        second_product(edge_values(sums_a[:], EDGES_A), EDGES_A, FIRST_BANKS)
-        split = PACK * width(EDGES_B)
-        sums_bc = keep.tile([P, split + PACK * width(EDGES_C)], F32, name="pre_mid", tag="from_src_0", align_bytes=64)
-        z_b = edge_values(sums_bc[:, :split].rearrange("p (t n) -> p t n", t=PACK), EDGES_B)
-        z_c = edge_values(sums_bc[:, split:].rearrange("p (t n) -> p t n", t=PACK), EDGES_C)
-        sums_d = keep.tile([P, PACK, width(EDGES_D)], F32, name="pre_last", tag="z_0", align_bytes=64)
-        z_d = edge_values(sums_d[:], EDGES_D)
+        z_a = edge_values(sums_a[:], EDGES_A, in_order)
+        start_b = PACK * BANK - (PACK - 1) * width(EDGES_B) + width(EDGES_B) // 2
+        sums_b = src_low[:, start_b : start_b + PACK * width(EDGES_B)]
+        z_b = edge_values(sums_b.rearrange("p (t n) -> p t n", t=PACK), EDGES_B, last_first)
+        z_c = edge_values(from_src[1][:, :, : width(EDGES_C)], EDGES_C, last_first)
+        second_product(quantise_edges(z_a, EDGES_A, 2), EDGES_A, FIRST_BANKS)
+        sums_d = z_a[:, : 2 * PACK * width(EDGES_D)].bitcast(F32)
+        z_d = edge_values(sums_d.rearrange("p (t n) -> p t n", t=PACK), EDGES_D, in_order)
         for n, (z, edges) in enumerate(((z_b, EDGES_B), (z_c, EDGES_C), (z_d, EDGES_D))):
-            second_product(z, edges, FIRST_BANKS + 1 + n)
+            second_product(quantise_edges(z, edges, 1), edges, FIRST_BANKS + 1 + n)

@@ -130,11 +130,21 @@ def tile_picked_hub_silu_e_kernel(tc, xT, w1, w2, w3, offs, src, dst, out):
         quantise_weights([(0, 1)], slots[0])
         quantise_weights([(0, 2)], slots[1])
 
-        rows = {(side, t): keep.tile([P, S], F32, name=f"rows_{side}_{t}") for side in range(2) for t in range(PACK)}
-        src_low = keep.tile([P, (PACK + 1) * BANK], F32, name="src_low")
-        src_high = keep.tile([P, PACK * BANK], F32, name="src_high")
-        from_src = [half[:, : PACK * BANK].rearrange("p (t n) -> p t n", t=PACK) for half in (src_low, src_high)]
-        order = [(side, t) for side in range(2) for t in range(PACK)]
+        y_all = keep.tile([P, PACK * S], F32, name="y_all")
+        rows = {(0, t): y_all[:, (PACK - 1 - t) * S : (PACK - t) * S] for t in range(PACK)}
+        for t in range(PACK):
+            rows[1, t] = keep.tile([P, S], F32, name=f"e_{t}")[:]
+        margin = (EDGES_B[1] - EDGES_B[0]) * 3 // 2
+        src_apart = keep.tile([P, 2 * BANK], F32, name="src_apart")
+        src_rest = keep.tile([P, PACK * U - BANK], F32, name="src_rest")
+
+        def from_src(t, a, b):
+            if t == 0 and a < BANK:
+                return src_apart[:, margin + a : margin + b]
+            return src_rest[:, t * U - BANK + a : t * U - BANK + b]
+
+        last_e = [*range(1, PACK), 0]
+        order = [(0, t) for t in range(PACK)] + [(1, t) for t in last_e]
         for n, (side, t) in enumerate(order):
             if n + 2 < len(order) and order[n + 2] not in weights:
                 ahead = order[n + 2]
@@ -146,9 +156,12 @@ def tile_picked_hub_silu_e_kernel(tc, xT, w1, w2, w3, offs, src, dst, out):
             else:
                 banks = [(2 * n - 2) % FIRST_BANKS, (2 * n - 1) % FIRST_BANKS]
                 first_product(rows[side, t], codes, scales, HALVES, banks)
-            if side == 0:
-                for half, (a, b) in zip(from_src, HALVES):
-                    nc.vector.tensor_copy(half[:, t, :], rows[0, t][:].indirect(entries(src_t, a, b)))
+            if n == 0:
+                for a, b in HALVES:
+                    nc.vector.tensor_copy(from_src(t, a, b), rows[0, t].indirect(entries(src_t, a, b)))
+            elif side == 0:
+                window = y_all[:, (PACK - 1 - t) * S : (PACK + 1 - t) * S]
+                nc.vector.tensor_copy(from_src(t, 0, U), window.indirect(src_t[:]))
 
         w3_grouped = keep.tile([P, N * PACK], BF16, name="w3_grouped", align_bytes=64)
         nc.scalar.copy(
@@ -159,17 +172,11 @@ def tile_picked_hub_silu_e_kernel(tc, xT, w1, w2, w3, offs, src, dst, out):
         w3_scales = keep.tile([P, N], U8, name="w3_scales", align_bytes=64)
         nc.vector.quantize_mx(out=w3_codes[:].bitcast(FP8X4), scales=w3_scales[:], in_=w3_grouped[:])
 
-        def quantise_edges(z, edges, cuts):
+        def quantise_edges(z, edges):
             a, b = edges
             z_codes = keep.tile([P, b - a], U32, name=f"zc_{a}", align_bytes=64)
             z_scales = keep.tile([P, b - a], U8, name=f"zs_{a}", align_bytes=64)
-            step = (b - a) // cuts
-            for lo in range(0, b - a, step):
-                nc.vector.quantize_mx(
-                    out=z_codes[:, lo : lo + step].bitcast(FP8X4),
-                    scales=z_scales[:, lo : lo + step],
-                    in_=z[:, PACK * lo : PACK * (lo + step)],
-                )
+            nc.vector.quantize_mx(out=z_codes[:].bitcast(FP8X4), scales=z_scales[:], in_=z[:])
             return z_codes, z_scales
 
         def second_product(quantised, edges, number):
@@ -191,12 +198,11 @@ def tile_picked_hub_silu_e_kernel(tc, xT, w1, w2, w3, offs, src, dst, out):
 
         def edge_values(sums, edges, tiles):
             a, b = edges
-            half = a // BANK
             for t in tiles:
                 nc.vector.tensor_tensor(
                     sums[:, t, :],
-                    rows[1, t][:].indirect(entries(dst_t, a, b)),
-                    from_src[half][:, t, a - BANK * half : b - BANK * half],
+                    rows[1, t].indirect(entries(dst_t, a, b)),
+                    from_src(t, a, b),
                     ADD,
                 )
             z = keep.tile([P, (b - a) * PACK], BF16, name=f"z_{a}", align_bytes=64)
@@ -211,15 +217,12 @@ def tile_picked_hub_silu_e_kernel(tc, xT, w1, w2, w3, offs, src, dst, out):
             return edges[1] - edges[0]
 
         in_order = range(PACK)
-        last_first = [PACK - 1, *range(PACK - 1)]
-        sums_a = keep.tile([P, PACK, width(EDGES_A)], F32, name="pre_first")
-        z_a = edge_values(sums_a[:], EDGES_A, in_order)
-        start_b = PACK * BANK - (PACK - 1) * width(EDGES_B) + width(EDGES_B) // 2
-        sums_b = src_low[:, start_b : start_b + PACK * width(EDGES_B)]
-        z_b = edge_values(sums_b.rearrange("p (t n) -> p t n", t=PACK), EDGES_B, last_first)
-        z_c = edge_values(from_src[1][:, :, : width(EDGES_C)], EDGES_C, last_first)
-        second_product(quantise_edges(z_a, EDGES_A, 2), EDGES_A, FIRST_BANKS)
-        sums_d = z_a[:, : 2 * PACK * width(EDGES_D)].bitcast(F32)
-        z_d = edge_values(sums_d.rearrange("p (t n) -> p t n", t=PACK), EDGES_D, in_order)
+        sums_a = keep.tile([P, PACK, width(EDGES_A)], F32, name="sums_a")
+        z_a = edge_values(sums_a[:], EDGES_A, last_e)
+        z_b = edge_values(src_apart[:].rearrange("p (t n) -> p t n", t=PACK), EDGES_B, in_order)
+        high_halves = src_rest[:].rearrange("p (t n) -> p t n", n=BANK)[:, ::2, :]
+        z_c = edge_values(high_halves[:, :, : width(EDGES_C)], EDGES_C, in_order)
+        second_product(quantise_edges(z_a, EDGES_A), EDGES_A, FIRST_BANKS)
+        z_d = edge_values(sums_a[:, :, : width(EDGES_D)], EDGES_D, in_order)
         for n, (z, edges) in enumerate(((z_b, EDGES_B), (z_c, EDGES_C), (z_d, EDGES_D))):
-            second_product(quantise_edges(z, edges, 1), edges, FIRST_BANKS + 1 + n)
+            second_product(quantise_edges(z, edges), edges, FIRST_BANKS + 1 + n)

@@ -27,7 +27,8 @@ VECTOR_SIXTEENTHS = [(10, 10, 10), (9, 11, 11)]
 NODE_QUARTERS = [(0, 256), (256, 512), (512, 768), (768, 1024)]
 HALVES = [(0, BANK), (BANK, 2 * BANK)]
 FIRST_BANKS = 4
-EDGES_A, EDGES_B, EDGES_C, EDGES_D = (0, 512), (512, 768), (768, 896), (896, 1024)
+EDGES_A, EDGES_B, EDGES_C, EDGES_D = (0, 512), (512, 768), (768, 928), (928, 1024)
+LAST_PRODUCTS = [(768, 896), (896, 1024)]
 
 
 def tile_picked_hub_silu_e_kernel(tc, xT, w1, w2, w3, offs, src, dst, out):
@@ -172,31 +173,33 @@ def tile_picked_hub_silu_e_kernel(tc, xT, w1, w2, w3, offs, src, dst, out):
         w3_scales = keep.tile([P, N], U8, name="w3_scales", align_bytes=64)
         nc.vector.quantize_mx(out=w3_codes[:].bitcast(FP8X4), scales=w3_scales[:], in_=w3_grouped[:])
 
-        def quantise_edges(z, edges):
+        def quantise_edges(edges):
             a, b = edges
             z_codes = keep.tile([P, b - a], U32, name=f"zc_{a}", align_bytes=64)
             z_scales = keep.tile([P, b - a], U8, name=f"zs_{a}", align_bytes=64)
-            nc.vector.quantize_mx(out=z_codes[:].bitcast(FP8X4), scales=z_scales[:], in_=z[:])
-            return z_codes, z_scales
+            nc.vector.quantize_mx(out=z_codes[:].bitcast(FP8X4), scales=z_scales[:], in_=z_of(edges))
+            return z_codes[:], z_scales[:]
 
-        def second_product(quantised, edges, number):
-            a, b = edges
-            z_codes, z_scales = quantised
-            acc = bank(number, "acc_out")
+        def second_product(z_codes, z_scales, number):
+            acc = bank(number, "acc_out")[:, : z_codes.shape[1]]
             nc.tensor.matmul_mx(
-                out=acc[:, : b - a],
+                out=acc,
                 lhsT=w3_codes[:].bitcast(FP8X4),
                 lhsT_scale=w3_scales[:],
-                rhs=z_codes[:].bitcast(FP8X4),
-                rhs_scale=z_scales[:],
+                rhs=z_codes.bitcast(FP8X4),
+                rhs_scale=z_scales,
                 start=True,
                 stop=True,
             )
-            done = keep.tile([P, b - a], F32, name=f"done_{a}")
-            nc.scalar.copy(done[:], acc[:, : b - a])
-            nc.sync.dma_start(out[:, a:b], done[:])
+            return acc
 
-        def edge_values(sums, edges, tiles):
+        def store(acc, first, engine_copy):
+            last = first + acc.shape[1]
+            done = keep.tile([P, last - first], F32, name=f"done_{first}")
+            engine_copy(done[:], acc)
+            nc.sync.dma_start(out[:, first:last], done[:])
+
+        def edge_values(z, sums, edges, tiles):
             a, b = edges
             for t in tiles:
                 nc.vector.tensor_tensor(
@@ -205,24 +208,31 @@ def tile_picked_hub_silu_e_kernel(tc, xT, w1, w2, w3, offs, src, dst, out):
                     from_src(t, a, b),
                     ADD,
                 )
-            z = keep.tile([P, (b - a) * PACK], BF16, name=f"z_{a}", align_bytes=64)
             nc.scalar.activation(
-                z[:].rearrange("p (c i t) -> p c t i", i=RUN, t=PACK),
+                z.rearrange("p (c i t) -> p c t i", i=RUN, t=PACK),
                 sums.rearrange("p t (c i) -> p c t i", i=RUN),
                 SILU,
             )
-            return z
+
+        z_all = keep.tile([P, U * PACK], BF16, name="z_all", align_bytes=64)
+
+        def z_of(edges):
+            return z_all[:, PACK * edges[0] : PACK * edges[1]]
 
         def width(edges):
             return edges[1] - edges[0]
 
         in_order = range(PACK)
         sums_a = keep.tile([P, PACK, width(EDGES_A)], F32, name="sums_a")
-        z_a = edge_values(sums_a[:], EDGES_A, last_e)
-        z_b = edge_values(src_apart[:].rearrange("p (t n) -> p t n", t=PACK), EDGES_B, in_order)
+        edge_values(z_of(EDGES_A), sums_a[:], EDGES_A, last_e)
+        edge_values(z_of(EDGES_B), src_apart[:].rearrange("p (t n) -> p t n", t=PACK), EDGES_B, in_order)
         high_halves = src_rest[:].rearrange("p (t n) -> p t n", n=BANK)[:, ::2, :]
-        z_c = edge_values(high_halves[:, :, : width(EDGES_C)], EDGES_C, in_order)
-        second_product(quantise_edges(z_a, EDGES_A), EDGES_A, FIRST_BANKS)
-        z_d = edge_values(sums_a[:, :, : width(EDGES_D)], EDGES_D, in_order)
-        for n, (z, edges) in enumerate(((z_b, EDGES_B), (z_c, EDGES_C), (z_d, EDGES_D))):
-            second_product(quantise_edges(z, edges), edges, FIRST_BANKS + 1 + n)
+        edge_values(z_of(EDGES_C), high_halves[:, :, : width(EDGES_C)], EDGES_C, in_order)
+        codes_a, scales_a = quantise_edges(EDGES_A)
+        half_a = width(EDGES_A) // 2
+        store(second_product(codes_a[:, :half_a], scales_a[:, :half_a], FIRST_BANKS), 0, nc.scalar.copy)
+        late_a = second_product(codes_a[:, half_a:], scales_a[:, half_a:], 0)
+        edge_values(z_of(EDGES_D), sums_a[:, :, : width(EDGES_D)], EDGES_D, in_order)
+        store(late_a, half_a, nc.vector.tensor_copy)
+        for n, edges in enumerate([EDGES_B, *LAST_PRODUCTS]):
+            store(second_product(*quantise_edges(edges), FIRST_BANKS + 1 + n), edges[0], nc.scalar.copy)

@@ -19,10 +19,11 @@ PACK = 4
 LIST_ROWS = 16
 BANK = 512
 BLOCK_ROWS = 8
+EDGES_A_LINE = 2
 RUN = 4
 
-X_CUTS = [(0, 896, 1664, 2048), (0, 768, 1536, 2048)]
-VECTOR_SIXTEENTHS = [(10, 10, 10), (9, 11, 11)]
+X_CUTS = [(0, 1280, 2048), (0, 768, 1536, 2048)]
+VECTOR_SIXTEENTHS = [(10, 11), (8, 11, 11)]
 
 NODE_QUARTERS = [(0, 256), (256, 512), (512, 768), (768, 1024)]
 HALVES = [(0, BANK), (BANK, 2 * BANK)]
@@ -209,8 +210,8 @@ def tile_picked_hub_silu_e_kernel(tc, xT, w1, w2, w3, offs, src, dst, out):
                     ADD,
                 )
             nc.scalar.activation(
-                z.rearrange("p (c i t) -> p c t i", i=RUN, t=PACK),
-                sums.rearrange("p t (c i) -> p c t i", i=RUN),
+                z.rearrange("p (c i t) -> p c t i", i=EDGES_A_LINE, t=PACK),
+                sums.rearrange("p t (c i) -> p c t i", i=EDGES_A_LINE),
                 SILU,
             )
 

@@ -19,7 +19,7 @@ PACK = 4
 LIST_ROWS = 16
 BANK = 512
 BLOCK_ROWS = 8
-EDGES_A_LINE = 2
+LINE_COLUMNS = 2
 RUN = 4
 
 X_CUTS = [(0, 1280, 2048), (0, 768, 1536, 2048)]
@@ -87,10 +87,10 @@ def tile_picked_hub_silu_e_kernel(tc, xT, w1, w2, w3, offs, src, dst, out):
 
         weights = {}
 
-        def group_weights(side, t, engine_copy, grouped):
+        def group_weights(side, t, engine_copy, run, grouped):
             engine_copy(
-                grouped.rearrange("p (b g i j) -> p b g j i", g=BLOCK_ROWS // RUN, i=RUN, j=PACK),
-                w_raw[side].rearrange("p j (b t g i) -> p t b g j i", t=PACK, g=BLOCK_ROWS // RUN, i=RUN)[:, t],
+                grouped.rearrange("p (b g i j) -> p b g j i", g=BLOCK_ROWS // run, i=run, j=PACK),
+                w_raw[side].rearrange("p j (b t g i) -> p t b g j i", t=PACK, g=BLOCK_ROWS // run, i=run)[:, t],
             )
 
         def quantise_weights(tiles, grouped):
@@ -102,7 +102,7 @@ def tile_picked_hub_silu_e_kernel(tc, xT, w1, w2, w3, offs, src, dst, out):
                 weights[key] = (codes[:, n * P : (n + 1) * P], scales[:, n * P : (n + 1) * P])
 
         first_grouped = keep.tile([P, P * PACK], BF16, name="first_grouped", align_bytes=64)
-        group_weights(0, 0, nc.scalar.copy, first_grouped[:])
+        group_weights(0, 0, nc.scalar.copy, LINE_COLUMNS, first_grouped[:])
         quantise_weights([(0, 0)], first_grouped[:])
 
         x_codes = keep.tile([P, S], U32, name="x_codes", align_bytes=64)
@@ -127,8 +127,8 @@ def tile_picked_hub_silu_e_kernel(tc, xT, w1, w2, w3, offs, src, dst, out):
                 nc.scalar.copy(result[:, a:b], acc[:, : b - a])
 
         slots = [picked[:, u, NODE_QUARTERS[-1][0] :].bitcast(BF16) for u in range(2)]
-        group_weights(0, 1, nc.vector.tensor_copy, slots[0])
-        group_weights(0, 2, nc.vector.tensor_copy, slots[1])
+        group_weights(0, 1, nc.vector.tensor_copy, RUN, slots[0])
+        group_weights(0, 2, nc.vector.tensor_copy, RUN, slots[1])
         quantise_weights([(0, 1)], slots[0])
         quantise_weights([(0, 2)], slots[1])
 
@@ -150,7 +150,7 @@ def tile_picked_hub_silu_e_kernel(tc, xT, w1, w2, w3, offs, src, dst, out):
         for n, (side, t) in enumerate(order):
             if n + 2 < len(order) and order[n + 2] not in weights:
                 ahead = order[n + 2]
-                group_weights(ahead[0], ahead[1], nc.scalar.copy, slots[(n + 1) % 2])
+                group_weights(ahead[0], ahead[1], nc.scalar.copy, LINE_COLUMNS, slots[(n + 1) % 2])
                 quantise_weights([ahead], slots[(n + 1) % 2])
             codes, scales = weights[side, t]
             if n == 0:
@@ -167,8 +167,8 @@ def tile_picked_hub_silu_e_kernel(tc, xT, w1, w2, w3, offs, src, dst, out):
 
         w3_grouped = keep.tile([P, N * PACK], BF16, name="w3_grouped", align_bytes=64)
         nc.scalar.copy(
-            w3_grouped[:].rearrange("p (c i t) -> p c t i", i=RUN, t=PACK),
-            w3_raw[:].rearrange("p t (c i) -> p c t i", i=RUN),
+            w3_grouped[:].rearrange("p (c i t) -> p c t i", i=LINE_COLUMNS, t=PACK),
+            w3_raw[:].rearrange("p t (c i) -> p c t i", i=LINE_COLUMNS),
         )
         w3_codes = keep.tile([P, N], U32, name="w3_codes", align_bytes=64)
         w3_scales = keep.tile([P, N], U8, name="w3_scales", align_bytes=64)
@@ -210,8 +210,8 @@ def tile_picked_hub_silu_e_kernel(tc, xT, w1, w2, w3, offs, src, dst, out):
                     ADD,
                 )
             nc.scalar.activation(
-                z.rearrange("p (c i t) -> p c t i", i=EDGES_A_LINE, t=PACK),
-                sums.rearrange("p t (c i) -> p c t i", i=EDGES_A_LINE),
+                z.rearrange("p (c i t) -> p c t i", i=LINE_COLUMNS, t=PACK),
+                sums.rearrange("p t (c i) -> p c t i", i=LINE_COLUMNS),
                 SILU,
             )
 

@@ -12,6 +12,7 @@ U16 = mybir.dt.uint16
 U8 = mybir.dt.uint8
 FP8X4 = mybir.dt.float8_e4m3fn_x4
 ADD = mybir.AluOpType.add
+COPY = mybir.ActivationFunctionType.Copy
 SILU = mybir.ActivationFunctionType.Silu
 
 P = 128
@@ -22,8 +23,8 @@ BLOCK_ROWS = 8
 LINE_COLUMNS = 2
 RUN = 4
 
-X_CUTS = [(0, 1280, 2048), (0, 768, 1536, 2048)]
-VECTOR_SIXTEENTHS = [(10, 11), (8, 11, 11)]
+SCALAR_FROM = 768
+ROW_ORDER = (0, 2, 1, 3)
 
 NODE_QUARTERS = [(0, 256), (256, 512), (512, 768), (768, 1024)]
 HALVES = [(0, BANK), (BANK, 2 * BANK)]
@@ -48,49 +49,43 @@ def tile_picked_hub_silu_e_kernel(tc, xT, w1, w2, w3, offs, src, dst, out):
         def entries(list_tile, a, b):
             return list_tile[:, a // LIST_ROWS : b // LIST_ROWS]
 
-        x_rows = xT.rearrange("(p u e) n -> u p (e n)", u=2, e=2)
-        raw = [keep.tile([P, 2 * T], F32, name=f"raw_{u}") for u in range(2)]
-        for u in range(2):
-            for a, b in zip(X_CUTS[u], X_CUTS[u][1:]):
-                start = T + a if a else 0
-                nc.sync.dma_start(raw[u][:, start : T + b], x_rows[u][:, start : T + b])
-                if u == 0 and a == 0:
-                    nc.sync.dma_start(offs_t[:], offs)
+        x_rows = xT.rearrange("(p j) n -> j p n", j=PACK)
+        raw = [keep.tile([P, T], F32, name=f"raw_{j}") for j in range(PACK)]
+        nc.sync.dma_start(offs_t[:], offs)
+        for j in ROW_ORDER:
+            nc.sync.dma_start(raw[j][:], x_rows[j])
         w_raw = []
+        w_tiles = []
         for name, w, list_tile, list_in in (("w1", w1, src_t, src), ("w2", w2, dst_t, dst)):
-            tile_w = keep.tile([P, PACK, H], F32, name=f"{name}_raw")
-            nc.sync.dma_start(tile_w[:], w.rearrange("(p j) c -> p j c", j=PACK))
-            w_raw.append(tile_w[:])
+            front = 2 * 256 - BLOCK_ROWS if name == "w1" else 0
+            tile_w = keep.tile([P, front + PACK * H], F32, name=f"{name}_raw", align_bytes=64)
+            nc.sync.dma_start(tile_w[:, front:], w.rearrange("(p j) c -> p (j c)", j=PACK))
+            w_raw.append(tile_w[:, front:].rearrange("p (j c) -> p j c", j=PACK))
+            w_tiles.append(tile_w)
             nc.sync.dma_start(list_tile[:], list_in)
         w3_raw = keep.tile([P, PACK, N], F32, name="w3_raw")
         w3_rows = w3.rearrange("(b t q) n -> t b q n", t=PACK, q=BLOCK_ROWS)
         for t in range(PACK):
             nc.sync.dma_start(w3_raw[:, t, :], w3_rows[t])
 
-        pairs = [keep.tile([P, T * 2], BF16, name=f"pairs_{u}", align_bytes=64) for u in range(2)]
-
-        def round_pairs(engine_copy, u, lo, hi):
-            engine_copy(
-                pairs[u][:, 2 * lo : 2 * hi].rearrange("p (n e) -> p n e", e=2),
-                raw[u][:].rearrange("p (e n) -> p n e", e=2)[:, lo:hi, :],
-            )
-
         picked_tile = keep.tile([P, 2 * S], U32, name="picked", align_bytes=64)
         picked = picked_tile[:].rearrange("p (u n) -> p u n", u=2)
-        for u in range(2):
-            for a, b, share in zip(X_CUTS[u], X_CUTS[u][1:], VECTOR_SIXTEENTHS[u]):
-                middle = a + (b - a) * share // 16
-                round_pairs(nc.vector.tensor_copy, u, a, middle)
-                round_pairs(nc.scalar.copy, u, middle, b)
-            for a, b in NODE_QUARTERS if u else [(0, S)]:
-                nc.vector.tensor_copy(picked[:, u, a:b], pairs[u][:].bitcast(U32).indirect(entries(offs_t, a, b)))
+        picked_rows = picked_tile[:].bitcast(BF16).rearrange("p (u n e) -> p u e n", u=2, e=2)
+        for j in ROW_ORDER:
+            row = picked_rows[:, j // 2, j % 2]
+            if j < 2:
+                rounded = keep.tile([P, T], BF16, name=f"rounded_{j}", align_bytes=64)
+                nc.scalar.copy(rounded[:], raw[j][:])
+                nc.scalar.activation(row[:, SCALAR_FROM:], rounded[:].indirect(entries(offs_t, SCALAR_FROM, S)), COPY)
+            for a, b in [[(0, SCALAR_FROM)], [(0, SCALAR_FROM)], [(0, S)], NODE_QUARTERS][j]:
+                nc.vector.tensor_copy(row[:, a:b], raw[j][:].indirect(entries(offs_t, a, b)))
 
         weights = {}
 
-        def group_weights(side, t, engine_copy, run, grouped):
+        def group_weights(side, t, engine_copy, run, grouped, lo=0, hi=P // BLOCK_ROWS):
             engine_copy(
-                grouped.rearrange("p (b g i j) -> p b g j i", g=BLOCK_ROWS // run, i=run, j=PACK),
-                w_raw[side].rearrange("p j (b t g i) -> p t b g j i", t=PACK, g=BLOCK_ROWS // run, i=run)[:, t],
+                grouped.rearrange("p (b g i j) -> p b g j i", g=BLOCK_ROWS // run, i=run, j=PACK)[:, lo:hi],
+                w_raw[side].rearrange("p j (b t g i) -> p t b g j i", t=PACK, g=BLOCK_ROWS // run, i=run)[:, t, lo:hi],
             )
 
         def quantise_weights(tiles, grouped):
@@ -102,13 +97,17 @@ def tile_picked_hub_silu_e_kernel(tc, xT, w1, w2, w3, offs, src, dst, out):
                 weights[key] = (codes[:, n * P : (n + 1) * P], scales[:, n * P : (n + 1) * P])
 
         first_grouped = keep.tile([P, P * PACK], BF16, name="first_grouped", align_bytes=64)
-        group_weights(0, 0, nc.scalar.copy, LINE_COLUMNS, first_grouped[:])
+        group_weights(0, 0, nc.scalar.copy, LINE_COLUMNS, first_grouped[:], 0, 8)
+        group_weights(0, 0, nc.scalar.copy, LINE_COLUMNS, first_grouped[:], 8, 16)
         quantise_weights([(0, 0)], first_grouped[:])
 
         x_codes = keep.tile([P, S], U32, name="x_codes", align_bytes=64)
         x_scales = keep.tile([P, S], U8, name="x_scales", align_bytes=64)
         for a, b in NODE_QUARTERS:
-            woven = keep.tile([P, (b - a) * 2], U32, name=f"woven_{a}", align_bytes=64)[:]
+            if b == S:
+                woven = w_tiles[0][:, : (b - a) * 2].bitcast(U32)
+            else:
+                woven = keep.tile([P, (b - a) * 2], U32, name=f"woven_{a}", align_bytes=64)[:]
             nc.scalar.copy(woven.rearrange("p (n u) -> p n u", u=2), picked[:, :, a:b].rearrange("p u n -> p n u"))
             nc.vector.quantize_mx(out=x_codes[:, a:b].bitcast(FP8X4), scales=x_scales[:, a:b], in_=woven.bitcast(BF16))
 
@@ -148,10 +147,23 @@ def tile_picked_hub_silu_e_kernel(tc, xT, w1, w2, w3, offs, src, dst, out):
         last_e = [*range(1, PACK), 0]
         order = [(0, t) for t in range(PACK)] + [(1, t) for t in last_e]
         for n, (side, t) in enumerate(order):
-            if n + 2 < len(order) and order[n + 2] not in weights:
-                ahead = order[n + 2]
-                group_weights(ahead[0], ahead[1], nc.scalar.copy, LINE_COLUMNS, slots[(n + 1) % 2])
-                quantise_weights([ahead], slots[(n + 1) % 2])
+            if n in (1, 2):
+                group_weights(*order[n + 2], nc.scalar.copy, LINE_COLUMNS, slots[(n + 1) % 2])
+                quantise_weights([order[n + 2]], slots[(n + 1) % 2])
+            if n in (3, 4):
+                both = keep.tile([P, 2 * P * PACK], BF16, name=f"both_{n}", align_bytes=64)
+                first, second = both[:, : P * PACK], both[:, P * PACK :]
+                if n == 3:
+                    group_weights(*order[5], nc.scalar.copy, LINE_COLUMNS, first)
+                    group_weights(*order[6], nc.scalar.copy, LINE_COLUMNS, second)
+                    quantise_weights(order[5:7], both[:])
+                else:
+                    group_weights(*order[7], nc.scalar.copy, LINE_COLUMNS, first)
+                    nc.scalar.copy(
+                        second.rearrange("p (c i t) -> p c t i", i=LINE_COLUMNS, t=PACK),
+                        w3_raw[:].rearrange("p t (c i) -> p c t i", i=LINE_COLUMNS),
+                    )
+                    quantise_weights([order[7], "w3"], both[:])
             codes, scales = weights[side, t]
             if n == 0:
                 first_product(rows[side, t], codes, scales, NODE_QUARTERS, range(FIRST_BANKS))
@@ -165,15 +177,6 @@ def tile_picked_hub_silu_e_kernel(tc, xT, w1, w2, w3, offs, src, dst, out):
                 window = y_all[:, (PACK - 1 - t) * S : (PACK + 1 - t) * S]
                 nc.vector.tensor_copy(from_src(t, 0, U), window.indirect(src_t[:]))
 
-        w3_grouped = keep.tile([P, N * PACK], BF16, name="w3_grouped", align_bytes=64)
-        nc.scalar.copy(
-            w3_grouped[:].rearrange("p (c i t) -> p c t i", i=LINE_COLUMNS, t=PACK),
-            w3_raw[:].rearrange("p t (c i) -> p c t i", i=LINE_COLUMNS),
-        )
-        w3_codes = keep.tile([P, N], U32, name="w3_codes", align_bytes=64)
-        w3_scales = keep.tile([P, N], U8, name="w3_scales", align_bytes=64)
-        nc.vector.quantize_mx(out=w3_codes[:].bitcast(FP8X4), scales=w3_scales[:], in_=w3_grouped[:])
-
         def quantise_edges(edges):
             a, b = edges
             z_codes = keep.tile([P, b - a], U32, name=f"zc_{a}", align_bytes=64)
@@ -185,8 +188,8 @@ def tile_picked_hub_silu_e_kernel(tc, xT, w1, w2, w3, offs, src, dst, out):
             acc = bank(number, "acc_out")[:, : z_codes.shape[1]]
             nc.tensor.matmul_mx(
                 out=acc,
-                lhsT=w3_codes[:].bitcast(FP8X4),
-                lhsT_scale=w3_scales[:],
+                lhsT=weights["w3"][0].bitcast(FP8X4),
+                lhsT_scale=weights["w3"][1],
                 rhs=z_codes.bitcast(FP8X4),
                 rhs_scale=z_scales,
                 start=True,

@@ -23,10 +23,13 @@ BLOCK_ROWS = 8
 LINE_COLUMNS = 2
 RUN = 4
 
-SCALAR_FROM = 768
-ROW_ORDER = (0, 2, 1, 3)
+SCALAR_FROM = 704
+ROW_ORDER = (0, 1, 2, 3)
 
-NODE_QUARTERS = [(0, 256), (256, 512), (512, 768), (768, 1024)]
+NODE_QUARTERS = [(0, 256), (256, 512), (768, 1024), (512, 768)]
+LAST_QUARTER = 768
+VECTOR_PIECES = [(0, 384), (384, SCALAR_FROM)]
+MARGIN = 384
 HALVES = [(0, BANK), (BANK, 2 * BANK)]
 FIRST_BANKS = 4
 EDGES_A, EDGES_B, EDGES_C, EDGES_D = (0, 512), (512, 768), (768, 928), (928, 1024)
@@ -41,6 +44,10 @@ def tile_picked_hub_silu_e_kernel(tc, xT, w1, w2, w3, offs, src, dst, out):
 
         def bank(number, name):
             return psum.tile([P, BANK], F32, name=name, tag=f"bank_{number}")
+
+        warm = keep.tile([P, 2], F32, name="warm")
+        nc.vector.memset(warm[:, 0:1], 0.0)
+        nc.scalar.activation(warm[:, 1:2], warm[:, 0:1], SILU)
 
         offs_t = keep.tile([P, S // LIST_ROWS], U16, name="offs_t")
         src_t = keep.tile([P, U // LIST_ROWS], U16, name="src_t")
@@ -57,10 +64,11 @@ def tile_picked_hub_silu_e_kernel(tc, xT, w1, w2, w3, offs, src, dst, out):
         w_raw = []
         w_tiles = []
         for name, w, list_tile, list_in in (("w1", w1, src_t, src), ("w2", w2, dst_t, dst)):
-            front = 2 * 256 - BLOCK_ROWS if name == "w1" else 0
-            tile_w = keep.tile([P, front + PACK * H], F32, name=f"{name}_raw", align_bytes=64)
-            nc.sync.dma_start(tile_w[:, front:], w.rearrange("(p j) c -> p (j c)", j=PACK))
-            w_raw.append(tile_w[:, front:].rearrange("p (j c) -> p j c", j=PACK))
+            front = 2 * LAST_QUARTER - BLOCK_ROWS if name == "w1" else 0
+            back = 2 * BANK - MARGIN - BLOCK_ROWS if name == "w2" else 0
+            tile_w = keep.tile([P, front + PACK * H + back], F32, name=f"{name}_raw", align_bytes=64)
+            nc.sync.dma_start(tile_w[:, front : front + PACK * H], w.rearrange("(p j) c -> p (j c)", j=PACK))
+            w_raw.append(tile_w[:, front : front + PACK * H].rearrange("p (j c) -> p j c", j=PACK))
             w_tiles.append(tile_w)
             nc.sync.dma_start(list_tile[:], list_in)
         w3_raw = keep.tile([P, PACK, N], F32, name="w3_raw")
@@ -68,17 +76,22 @@ def tile_picked_hub_silu_e_kernel(tc, xT, w1, w2, w3, offs, src, dst, out):
         for t in range(PACK):
             nc.sync.dma_start(w3_raw[:, t, :], w3_rows[t])
 
-        picked_tile = keep.tile([P, 2 * S], U32, name="picked", align_bytes=64)
-        picked = picked_tile[:].rearrange("p (u n) -> p u n", u=2)
-        picked_rows = picked_tile[:].bitcast(BF16).rearrange("p (u n e) -> p u e n", u=2, e=2)
-        for j in ROW_ORDER:
-            row = picked_rows[:, j // 2, j % 2]
-            if j < 2:
-                rounded = keep.tile([P, T], BF16, name=f"rounded_{j}", align_bytes=64)
-                nc.scalar.copy(rounded[:], raw[j][:])
-                nc.scalar.activation(row[:, SCALAR_FROM:], rounded[:].indirect(entries(offs_t, SCALAR_FROM, S)), COPY)
-            for a, b in [[(0, SCALAR_FROM)], [(0, SCALAR_FROM)], [(0, S)], NODE_QUARTERS][j]:
-                nc.vector.tensor_copy(row[:, a:b], raw[j][:].indirect(entries(offs_t, a, b)))
+        woven = w_tiles[0][:, : 2 * LAST_QUARTER].bitcast(BF16)
+        woven_last = keep.tile([P, (S - LAST_QUARTER) * PACK], BF16, name="woven_last", align_bytes=64)
+        woven_rows = woven.rearrange("p (n j) -> p j n", j=PACK)
+        planes = keep.tile([P, PACK, S - SCALAR_FROM], BF16, name="planes", align_bytes=64)
+        for j in range(PACK):
+            nc.scalar.activation(planes[:, j, :], raw[j][:].indirect(entries(offs_t, SCALAR_FROM, S)), COPY)
+            for a, b in VECTOR_PIECES if j == PACK - 1 else [(0, SCALAR_FROM)]:
+                nc.vector.tensor_copy(woven_rows[:, j, a:b], raw[j][:].indirect(entries(offs_t, a, b)))
+
+        def interleave(target, a, b):
+            nc.scalar.copy(
+                target.rearrange("p (c i j) -> p c j i", i=LINE_COLUMNS, j=PACK),
+                planes[:, :, a - SCALAR_FROM : b - SCALAR_FROM].rearrange("p j (c i) -> p c j i", i=LINE_COLUMNS),
+            )
+
+        interleave(woven_last[:], LAST_QUARTER, S)
 
         weights = {}
 
@@ -96,20 +109,19 @@ def tile_picked_hub_silu_e_kernel(tc, xT, w1, w2, w3, offs, src, dst, out):
             for n, key in enumerate(tiles):
                 weights[key] = (codes[:, n * P : (n + 1) * P], scales[:, n * P : (n + 1) * P])
 
-        first_grouped = keep.tile([P, P * PACK], BF16, name="first_grouped", align_bytes=64)
-        group_weights(0, 0, nc.scalar.copy, LINE_COLUMNS, first_grouped[:], 0, 8)
-        group_weights(0, 0, nc.scalar.copy, LINE_COLUMNS, first_grouped[:], 8, 16)
-        quantise_weights([(0, 0)], first_grouped[:])
+        two_slots = keep.tile([P, 2 * P * PACK], BF16, name="two_slots", align_bytes=64)
+        first_grouped = two_slots[:, P * PACK // 2 : 3 * P * PACK // 2]
+        group_weights(0, 0, nc.scalar.copy, LINE_COLUMNS, first_grouped, 0, 8)
+        group_weights(0, 0, nc.scalar.copy, LINE_COLUMNS, first_grouped, 8, 16)
+        quantise_weights([(0, 0)], first_grouped)
+        interleave(woven[:, SCALAR_FROM * PACK :], SCALAR_FROM, LAST_QUARTER)
+        second_grouped = keep.tile([P, P * PACK], BF16, name="second_grouped", align_bytes=64)
+        group_weights(0, 1, nc.scalar.copy, LINE_COLUMNS, second_grouped[:])
 
         x_codes = keep.tile([P, S], U32, name="x_codes", align_bytes=64)
         x_scales = keep.tile([P, S], U8, name="x_scales", align_bytes=64)
         for a, b in NODE_QUARTERS:
-            if b == S:
-                woven = w_tiles[0][:, : (b - a) * 2].bitcast(U32)
-            else:
-                woven = keep.tile([P, (b - a) * 2], U32, name=f"woven_{a}", align_bytes=64)[:]
-            nc.scalar.copy(woven.rearrange("p (n u) -> p n u", u=2), picked[:, :, a:b].rearrange("p u n -> p n u"))
-            nc.vector.quantize_mx(out=x_codes[:, a:b].bitcast(FP8X4), scales=x_scales[:, a:b], in_=woven.bitcast(BF16))
+            nc.vector.quantize_mx(out=x_codes[:, a:b].bitcast(FP8X4), scales=x_scales[:, a:b], in_=woven_last[:] if b == S else woven[:, a * PACK : b * PACK])
 
         def first_product(result, codes, scales, cuts, banks):
             for (a, b), number in zip(cuts, banks):
@@ -125,18 +137,11 @@ def tile_picked_hub_silu_e_kernel(tc, xT, w1, w2, w3, offs, src, dst, out):
                 )
                 nc.scalar.copy(result[:, a:b], acc[:, : b - a])
 
-        slots = [picked[:, u, NODE_QUARTERS[-1][0] :].bitcast(BF16) for u in range(2)]
-        group_weights(0, 1, nc.vector.tensor_copy, RUN, slots[0])
-        group_weights(0, 2, nc.vector.tensor_copy, RUN, slots[1])
-        quantise_weights([(0, 1)], slots[0])
-        quantise_weights([(0, 2)], slots[1])
+        slots = [two_slots[:, u * P * PACK : (u + 1) * P * PACK] for u in range(2)]
 
-        y_all = keep.tile([P, PACK * S], F32, name="y_all")
-        rows = {(0, t): y_all[:, (PACK - 1 - t) * S : (PACK - t) * S] for t in range(PACK)}
-        for t in range(PACK):
-            rows[1, t] = keep.tile([P, S], F32, name=f"e_{t}")[:]
+        rows = {(side, t): keep.tile([P, S], F32, name=f"rows_{side}_{t}")[:] for side in range(2) for t in range(PACK)}
         margin = (EDGES_B[1] - EDGES_B[0]) * 3 // 2
-        src_apart = keep.tile([P, 2 * BANK], F32, name="src_apart")
+        src_apart = w_tiles[1][:, PACK * H - BLOCK_ROWS - MARGIN :]
         src_rest = keep.tile([P, PACK * U - BANK], F32, name="src_rest")
 
         def from_src(t, a, b):
@@ -147,35 +152,36 @@ def tile_picked_hub_silu_e_kernel(tc, xT, w1, w2, w3, offs, src, dst, out):
         last_e = [*range(1, PACK), 0]
         order = [(0, t) for t in range(PACK)] + [(1, t) for t in last_e]
         for n, (side, t) in enumerate(order):
-            if n in (1, 2):
-                group_weights(*order[n + 2], nc.scalar.copy, LINE_COLUMNS, slots[(n + 1) % 2])
-                quantise_weights([order[n + 2]], slots[(n + 1) % 2])
-            if n in (3, 4):
-                both = keep.tile([P, 2 * P * PACK], BF16, name=f"both_{n}", align_bytes=64)
-                first, second = both[:, : P * PACK], both[:, P * PACK :]
-                if n == 3:
-                    group_weights(*order[5], nc.scalar.copy, LINE_COLUMNS, first)
-                    group_weights(*order[6], nc.scalar.copy, LINE_COLUMNS, second)
-                    quantise_weights(order[5:7], both[:])
-                else:
-                    group_weights(*order[7], nc.scalar.copy, LINE_COLUMNS, first)
-                    nc.scalar.copy(
-                        second.rearrange("p (c i t) -> p c t i", i=LINE_COLUMNS, t=PACK),
-                        w3_raw[:].rearrange("p t (c i) -> p c t i", i=LINE_COLUMNS),
-                    )
-                    quantise_weights([order[7], "w3"], both[:])
+            if n == 1:
+                quantise_weights([(0, 1)], second_grouped[:])
+                for u in range(2):
+                    group_weights(0, 2 + u, nc.vector.tensor_copy, RUN, slots[u])
+                both = [keep.tile([P, 2 * P * PACK], BF16, name=f"both_{h}", align_bytes=64) for h in range(2)]
+                group_weights(*order[4], nc.vector.tensor_copy, RUN, both[0][:, : P * PACK])
+                quantise_weights([(0, 2), (0, 3)], two_slots[:])
+                group_weights(*order[5], nc.vector.tensor_copy, RUN, both[0][:, P * PACK :])
+                group_weights(*order[6], nc.vector.tensor_copy, RUN, both[1][:, : P * PACK])
+                quantise_weights(order[4:6], both[0][:])
+                group_weights(*order[7], nc.vector.tensor_copy, RUN, both[1][:, P * PACK :])
+                w3_grouped = keep.tile([P, P * PACK], BF16, name="w3_grouped", align_bytes=64)
+                nc.vector.tensor_copy(
+                    w3_grouped[:].rearrange("p (c i t) -> p c t i", i=RUN, t=PACK),
+                    w3_raw[:].rearrange("p t (c i) -> p c t i", i=RUN),
+                )
+                quantise_weights(order[6:8], both[1][:])
+            if n == 2:
+                quantise_weights(["w3"], w3_grouped[:])
             codes, scales = weights[side, t]
             if n == 0:
                 first_product(rows[side, t], codes, scales, NODE_QUARTERS, range(FIRST_BANKS))
             else:
                 banks = [(2 * n - 2) % FIRST_BANKS, (2 * n - 1) % FIRST_BANKS]
                 first_product(rows[side, t], codes, scales, HALVES, banks)
-            if n == 0:
-                for a, b in HALVES:
-                    nc.vector.tensor_copy(from_src(t, a, b), rows[0, t].indirect(entries(src_t, a, b)))
-            elif side == 0:
-                window = y_all[:, (PACK - 1 - t) * S : (PACK + 1 - t) * S]
-                nc.vector.tensor_copy(from_src(t, 0, U), window.indirect(src_t[:]))
+            for t in {1: (0, 1), 2: (2,), 3: (3,)}.get(n, ()):
+                nc.vector.tensor_copy(from_src(t, *EDGES_A), rows[0, t].indirect(entries(src_t, *EDGES_A)))
+        for a, b in (EDGES_B, (EDGES_C[0], U)):
+            for t in range(PACK):
+                nc.scalar.activation(from_src(t, a, b), rows[0, t].indirect(entries(src_t, a, b)), COPY)
 
         def quantise_edges(edges):
             a, b = edges
@@ -229,7 +235,7 @@ def tile_picked_hub_silu_e_kernel(tc, xT, w1, w2, w3, offs, src, dst, out):
         in_order = range(PACK)
         sums_a = keep.tile([P, PACK, width(EDGES_A)], F32, name="sums_a")
         edge_values(z_of(EDGES_A), sums_a[:], EDGES_A, last_e)
-        edge_values(z_of(EDGES_B), src_apart[:].rearrange("p (t n) -> p t n", t=PACK), EDGES_B, in_order)
+        edge_values(z_of(EDGES_B), src_apart.rearrange("p (t n) -> p t n", t=PACK), EDGES_B, in_order)
         high_halves = src_rest[:].rearrange("p (t n) -> p t n", n=BANK)[:, ::2, :]
         edge_values(z_of(EDGES_C), high_halves[:, :, : width(EDGES_C)], EDGES_C, in_order)
         codes_a, scales_a = quantise_edges(EDGES_A)

@@ -12,6 +12,7 @@ U16 = mybir.dt.uint16
 U8 = mybir.dt.uint8
 FP8X4 = mybir.dt.float8_e4m3fn_x4
 ADD = mybir.AluOpType.add
+MULT = mybir.AluOpType.mult
 COPY = mybir.ActivationFunctionType.Copy
 SILU = mybir.ActivationFunctionType.Silu
 
@@ -22,16 +23,13 @@ BANK = 512
 BLOCK_ROWS = 8
 LINE_COLUMNS = 2
 RUN = 4
+GROUPED = P * PACK
 
+KIB = 1024
 SCALAR_FROM = 704
-ROW_ORDER = (0, 1, 2, 3)
-
-NODE_QUARTERS = [(0, 256), (256, 512), (768, 1024), (512, 768)]
-LAST_QUARTER = 768
+NODE_QUARTERS = [(0, 256), (256, 512), (512, 768), (768, 1024)]
 VECTOR_PIECES = [(0, 384), (384, SCALAR_FROM)]
-MARGIN = 384
 HALVES = [(0, BANK), (BANK, 2 * BANK)]
-FIRST_BANKS = 4
 EDGES_A, EDGES_B, EDGES_C, EDGES_D = (0, 512), (512, 768), (768, 928), (928, 1024)
 LAST_PRODUCTS = [(768, 896), (896, 1024)]
 
@@ -40,6 +38,7 @@ def tile_picked_hub_silu_e_kernel(tc, xT, w1, w2, w3, offs, src, dst, out):
     nc = tc.nc
     with ExitStack() as ctx:
         keep = ctx.enter_context(tc.tile_pool(name="keep", bufs=1))
+        held = ctx.enter_context(tc.tile_pool(name="held", bufs=1))
         psum = ctx.enter_context(tc.psum_pool(name="psum", bufs=1))
 
         def bank(number, name):
@@ -53,135 +52,156 @@ def tile_picked_hub_silu_e_kernel(tc, xT, w1, w2, w3, offs, src, dst, out):
         src_t = keep.tile([P, U // LIST_ROWS], U16, name="src_t")
         dst_t = keep.tile([P, U // LIST_ROWS], U16, name="dst_t")
 
+        def width(edges):
+            return edges[1] - edges[0]
+
         def entries(list_tile, a, b):
             return list_tile[:, a // LIST_ROWS : b // LIST_ROWS]
 
         x_rows = xT.rearrange("(p j) n -> j p n", j=PACK)
         raw = [keep.tile([P, T], F32, name=f"raw_{j}") for j in range(PACK)]
         nc.sync.dma_start(offs_t[:], offs)
-        for j in ROW_ORDER:
+        for j in range(PACK):
             nc.sync.dma_start(raw[j][:], x_rows[j])
         w_raw = []
-        w_tiles = []
         for name, w, list_tile, list_in in (("w1", w1, src_t, src), ("w2", w2, dst_t, dst)):
-            front = 2 * LAST_QUARTER - BLOCK_ROWS if name == "w1" else 0
-            back = 2 * BANK - MARGIN - BLOCK_ROWS if name == "w2" else 0
-            tile_w = keep.tile([P, front + PACK * H + back], F32, name=f"{name}_raw", align_bytes=64)
-            nc.sync.dma_start(tile_w[:, front : front + PACK * H], w.rearrange("(p j) c -> p (j c)", j=PACK))
-            w_raw.append(tile_w[:, front : front + PACK * H].rearrange("p (j c) -> p j c", j=PACK))
-            w_tiles.append(tile_w)
+            w_tile = keep.tile([P, PACK * H], F32, name=f"{name}_raw", align_bytes=64)
+            nc.sync.dma_start(w_tile[:], w.rearrange("(p j) c -> p (j c)", j=PACK))
             nc.sync.dma_start(list_tile[:], list_in)
+            w_raw.append(w_tile[:])
         w3_raw = keep.tile([P, PACK, N], F32, name="w3_raw")
         w3_rows = w3.rearrange("(b t q) n -> t b q n", t=PACK, q=BLOCK_ROWS)
         for t in range(PACK):
             nc.sync.dma_start(w3_raw[:, t, :], w3_rows[t])
 
-        woven = w_tiles[0][:, : 2 * LAST_QUARTER].bitcast(BF16)
-        woven_last = keep.tile([P, (S - LAST_QUARTER) * PACK], BF16, name="woven_last", align_bytes=64)
-        woven_rows = woven.rearrange("p (n j) -> p j n", j=PACK)
+        woven = keep.tile([P, S * PACK], BF16, name="woven", align_bytes=64)
+        woven_rows = woven[:].rearrange("p (n j) -> p j n", j=PACK)
         planes = keep.tile([P, PACK, S - SCALAR_FROM], BF16, name="planes", align_bytes=64)
         for j in range(PACK):
             nc.scalar.activation(planes[:, j, :], raw[j][:].indirect(entries(offs_t, SCALAR_FROM, S)), COPY)
             for a, b in VECTOR_PIECES if j == PACK - 1 else [(0, SCALAR_FROM)]:
                 nc.vector.tensor_copy(woven_rows[:, j, a:b], raw[j][:].indirect(entries(offs_t, a, b)))
 
-        def interleave(target, a, b):
-            nc.scalar.copy(
-                target.rearrange("p (c i j) -> p c j i", i=LINE_COLUMNS, j=PACK),
-                planes[:, :, a - SCALAR_FROM : b - SCALAR_FROM].rearrange("p j (c i) -> p c j i", i=LINE_COLUMNS),
-            )
-
-        interleave(woven_last[:], LAST_QUARTER, S)
+        nc.scalar.copy(
+            woven[:, SCALAR_FROM * PACK :].rearrange("p (c i j) -> p c j i", i=LINE_COLUMNS, j=PACK),
+            planes[:].rearrange("p j (c i) -> p c j i", i=LINE_COLUMNS),
+        )
 
         weights = {}
 
         def group_weights(side, t, engine_copy, run, grouped, lo=0, hi=P // BLOCK_ROWS):
             engine_copy(
                 grouped.rearrange("p (b g i j) -> p b g j i", g=BLOCK_ROWS // run, i=run, j=PACK)[:, lo:hi],
-                w_raw[side].rearrange("p j (b t g i) -> p t b g j i", t=PACK, g=BLOCK_ROWS // run, i=run)[:, t, lo:hi],
+                w_raw[side].rearrange("p (j b t g i) -> p t b g j i", j=PACK, t=PACK, g=BLOCK_ROWS // run, i=run)[:, t, lo:hi],
             )
 
-        def quantise_weights(tiles, grouped):
-            name = f"{tiles[0][0]}_{tiles[0][1]}"
-            codes = keep.tile([P, len(tiles) * P], U32, name=f"wc_{name}", align_bytes=64)
-            scales = keep.tile([P, len(tiles) * P], U8, name=f"ws_{name}", align_bytes=64)
+        def gpsimd_round(target, source):
+            nc.gpsimd.tensor_scalar(target, source, 1.0, 0.0, MULT, ADD)
+
+        def group_on_gpsimd(side, t, grouped):
+            gpsimd_round(
+                grouped.rearrange("p (b q j) -> p b q j", q=BLOCK_ROWS, j=PACK),
+                w_raw[side].rearrange("p (j b t q) -> p t b q j", j=PACK, t=PACK, q=BLOCK_ROWS)[:, t],
+            )
+
+        def quantise_weights(keys, grouped):
+            name = f"{keys[0][0]}_{keys[0][1]}"
+            codes = keep.tile([P, len(keys) * P], U32, name=f"wc_{name}", align_bytes=64)
+            scales = keep.tile([P, len(keys) * P], U8, name=f"ws_{name}", align_bytes=64)
             nc.vector.quantize_mx(out=codes[:].bitcast(FP8X4), scales=scales[:], in_=grouped)
-            for n, key in enumerate(tiles):
+            for n, key in enumerate(keys):
                 weights[key] = (codes[:, n * P : (n + 1) * P], scales[:, n * P : (n + 1) * P])
 
-        two_slots = keep.tile([P, 2 * P * PACK], BF16, name="two_slots", align_bytes=64)
-        first_grouped = two_slots[:, P * PACK // 2 : 3 * P * PACK // 2]
-        group_weights(0, 0, nc.scalar.copy, LINE_COLUMNS, first_grouped, 0, 8)
-        group_weights(0, 0, nc.scalar.copy, LINE_COLUMNS, first_grouped, 8, 16)
-        quantise_weights([(0, 0)], first_grouped)
-        interleave(woven[:, SCALAR_FROM * PACK :], SCALAR_FROM, LAST_QUARTER)
-        second_grouped = keep.tile([P, P * PACK], BF16, name="second_grouped", align_bytes=64)
-        group_weights(0, 1, nc.scalar.copy, LINE_COLUMNS, second_grouped[:])
+        def slot(tile, n):
+            return tile[:, n * GROUPED : (n + 1) * GROUPED]
 
-        x_codes = keep.tile([P, S], U32, name="x_codes", align_bytes=64)
         x_scales = keep.tile([P, S], U8, name="x_scales", align_bytes=64)
-        for a, b in NODE_QUARTERS:
-            nc.vector.quantize_mx(out=x_codes[:, a:b].bitcast(FP8X4), scales=x_scales[:, a:b], in_=woven_last[:] if b == S else woven[:, a * PACK : b * PACK])
+        x_low = keep.tile([P, BANK], U32, name="x_low", align_bytes=64)
 
-        def first_product(result, codes, scales, cuts, banks):
-            for (a, b), number in zip(cuts, banks):
+        def x_codes(a, b):
+            return x_low[:, a:b] if a < BANK else x_high[:, a - BANK : b - BANK]
+
+        def quantise_nodes(a, b):
+            nc.vector.quantize_mx(out=x_codes(a, b).bitcast(FP8X4), scales=x_scales[:, a:b], in_=woven[:, a * PACK : b * PACK])
+
+        for a, b in NODE_QUARTERS[:2]:
+            quantise_nodes(a, b)
+        first_grouped = held.tile([P, GROUPED], BF16, name="first_grouped", offset=13 * KIB, align_bytes=64)
+        second_grouped = keep.tile([P, GROUPED], BF16, name="second_grouped", align_bytes=64)
+        group_weights(0, 0, nc.vector.tensor_copy, RUN, first_grouped[:])
+        group_weights(0, 1, nc.vector.tensor_copy, RUN, second_grouped[:])
+        quantise_weights([(0, 0)], first_grouped[:])
+        quantise_weights([(0, 1)], second_grouped[:])
+        x_high = held.tile([P, BANK], U32, name="x_high", offset=13 * KIB, align_bytes=64)
+        for a, b in NODE_QUARTERS[2:]:
+            quantise_nodes(a, b)
+        stage_y = held.tile([P, 2 * GROUPED], BF16, name="stage_y", offset=7 * KIB, align_bytes=64)
+        for n in range(2):
+            group_weights(0, 2 + n, nc.scalar.copy, LINE_COLUMNS, slot(stage_y, n))
+        quantise_weights([(0, 2), (0, 3)], stage_y[:])
+
+        rows = {(side, t): keep.tile([P, S], F32, name=f"rows_{side}_{t}")[:] for side in range(2) for t in range(PACK)}
+
+        def first_product(key, cuts, banks, copies):
+            codes, scales = weights[key]
+            for (a, b), number, engine_copy in zip(cuts, banks, copies):
                 acc = bank(number, "acc")
                 nc.tensor.matmul_mx(
                     out=acc[:, : b - a],
                     lhsT=codes.bitcast(FP8X4),
                     lhsT_scale=scales,
-                    rhs=x_codes[:, a:b].bitcast(FP8X4),
+                    rhs=x_codes(a, b).bitcast(FP8X4),
                     rhs_scale=x_scales[:, a:b],
                     start=True,
                     stop=True,
                 )
-                nc.scalar.copy(result[:, a:b], acc[:, : b - a])
+                engine_copy(rows[key][:, a:b], acc[:, : b - a])
 
-        slots = [two_slots[:, u * P * PACK : (u + 1) * P * PACK] for u in range(2)]
+        on_scalar, on_vector = nc.scalar.copy, nc.vector.tensor_copy
+        first_product((0, 0), NODE_QUARTERS, range(4), [on_scalar, on_scalar, on_scalar, on_vector])
 
-        rows = {(side, t): keep.tile([P, S], F32, name=f"rows_{side}_{t}")[:] for side in range(2) for t in range(PACK)}
-        margin = (EDGES_B[1] - EDGES_B[0]) * 3 // 2
-        src_apart = w_tiles[1][:, PACK * H - BLOCK_ROWS - MARGIN :]
-        src_rest = keep.tile([P, PACK * U - BANK], F32, name="src_rest")
+        early = {t: keep.tile([P, EDGES_B[1] if t == 0 else BANK], F32, name=f"early_{t}")[:] for t in range(3)}
+
+        def scalar_gather(target, t, a, b):
+            nc.scalar.activation(target, rows[0, t].indirect(entries(src_t, a, b)), COPY)
+
+        scalar_gather(early[0], 0, 0, EDGES_B[1])
+        for t, banks in ((1, (4, 5)), (2, (6, 7)), (3, (0, 1))):
+            first_product((0, t), HALVES, banks, [on_vector] * 2)
+            if t < 3:
+                scalar_gather(early[t], t, *EDGES_A)
+        stage_e = held.tile([P, PACK * GROUPED], BF16, name="stage_e", offset=7 * KIB, align_bytes=64)
+        for t in range(PACK):
+            group_on_gpsimd(1, t, slot(stage_e, t))
+        quantise_weights([(1, t) for t in range(PACK)], stage_e[:])
+        middle_3 = held.tile([P, width(EDGES_B)], F32, name="middle_3", offset=7 * KIB, align_bytes=64)
+        apart = held.tile([P, 2 * BANK], F32, name="apart", offset=9 * KIB, align_bytes=64)
+        stage_w3 = held.tile([P, GROUPED], BF16, name="stage_w3", offset=8 * KIB, align_bytes=64)
+        early[3] = apart[:, P : P + BANK]
+        gpsimd_round(stage_w3[:].rearrange("p (n t) -> p n t", t=PACK), w3_raw[:].rearrange("p t n -> p n t"))
+        nc.vector.tensor_copy(early[3], rows[0, 3].indirect(entries(src_t, *EDGES_A)))
+        nc.vector.tensor_copy(middle_3[:], rows[0, 3].indirect(entries(src_t, *EDGES_B)))
+        quantise_weights(["w3"], stage_w3[:])
+        for t, banks in enumerate([(2, 3), (4, 5), (6, 7), (0, 1)]):
+            first_product((1, t), HALVES, banks, [on_scalar] * 2)
+        late = held.tile([P, PACK, BANK], F32, name="late", offset=13 * KIB, align_bytes=64)
+        last_first = (3, 0, 1, 2)
+        for t in (1, 2):
+            scalar_gather(late[:, t, : width(EDGES_B)], t, *EDGES_B)
+        for t in last_first:
+            scalar_gather(late[:, t, width(EDGES_B) :], t, EDGES_C[0], U)
 
         def from_src(t, a, b):
-            if t == 0 and a < BANK:
-                return src_apart[:, margin + a : margin + b]
-            return src_rest[:, t * U - BANK + a : t * U - BANK + b]
+            if b <= early[t].shape[1]:
+                return early[t][:, a:b]
+            if t == 3 and (a, b) == EDGES_B:
+                return middle_3[:]
+            return late[:, t, a - BANK : b - BANK]
 
-        last_e = [*range(1, PACK), 0]
-        order = [(0, t) for t in range(PACK)] + [(1, t) for t in last_e]
-        for n, (side, t) in enumerate(order):
-            if n == 1:
-                quantise_weights([(0, 1)], second_grouped[:])
-                for u in range(2):
-                    group_weights(0, 2 + u, nc.vector.tensor_copy, RUN, slots[u])
-                both = [keep.tile([P, 2 * P * PACK], BF16, name=f"both_{h}", align_bytes=64) for h in range(2)]
-                group_weights(*order[4], nc.vector.tensor_copy, RUN, both[0][:, : P * PACK])
-                quantise_weights([(0, 2), (0, 3)], two_slots[:])
-                group_weights(*order[5], nc.vector.tensor_copy, RUN, both[0][:, P * PACK :])
-                group_weights(*order[6], nc.vector.tensor_copy, RUN, both[1][:, : P * PACK])
-                quantise_weights(order[4:6], both[0][:])
-                group_weights(*order[7], nc.vector.tensor_copy, RUN, both[1][:, P * PACK :])
-                w3_grouped = keep.tile([P, P * PACK], BF16, name="w3_grouped", align_bytes=64)
-                nc.vector.tensor_copy(
-                    w3_grouped[:].rearrange("p (c i t) -> p c t i", i=RUN, t=PACK),
-                    w3_raw[:].rearrange("p t (c i) -> p c t i", i=RUN),
-                )
-                quantise_weights(order[6:8], both[1][:])
-            if n == 2:
-                quantise_weights(["w3"], w3_grouped[:])
-            codes, scales = weights[side, t]
-            if n == 0:
-                first_product(rows[side, t], codes, scales, NODE_QUARTERS, range(FIRST_BANKS))
-            else:
-                banks = [(2 * n - 2) % FIRST_BANKS, (2 * n - 1) % FIRST_BANKS]
-                first_product(rows[side, t], codes, scales, HALVES, banks)
-            for t in {1: (0, 1), 2: (2,), 3: (3,)}.get(n, ()):
-                nc.vector.tensor_copy(from_src(t, *EDGES_A), rows[0, t].indirect(entries(src_t, *EDGES_A)))
-        for a, b in (EDGES_B, (EDGES_C[0], U)):
-            for t in range(PACK):
-                nc.scalar.activation(from_src(t, a, b), rows[0, t].indirect(entries(src_t, a, b)), COPY)
+        z_all = keep.tile([P, U * PACK], BF16, name="z_all", align_bytes=64)
+
+        def z_of(edges):
+            return z_all[:, PACK * edges[0] : PACK * edges[1]]
 
         def quantise_edges(edges):
             a, b = edges
@@ -209,40 +229,25 @@ def tile_picked_hub_silu_e_kernel(tc, xT, w1, w2, w3, offs, src, dst, out):
             engine_copy(done[:], acc)
             nc.sync.dma_start(out[:, first:last], done[:])
 
-        def edge_values(z, sums, edges, tiles):
+        def edge_values(sums, edges, tiles):
             a, b = edges
             for t in tiles:
-                nc.vector.tensor_tensor(
-                    sums[:, t, :],
-                    rows[1, t].indirect(entries(dst_t, a, b)),
-                    from_src(t, a, b),
-                    ADD,
-                )
+                nc.vector.tensor_tensor(sums[:, t, :], rows[1, t].indirect(entries(dst_t, a, b)), from_src(t, a, b), ADD)
             nc.scalar.activation(
-                z.rearrange("p (c i t) -> p c t i", i=LINE_COLUMNS, t=PACK),
+                z_of(edges).rearrange("p (c i t) -> p c t i", i=LINE_COLUMNS, t=PACK),
                 sums.rearrange("p t (c i) -> p c t i", i=LINE_COLUMNS),
                 SILU,
             )
 
-        z_all = keep.tile([P, U * PACK], BF16, name="z_all", align_bytes=64)
-
-        def z_of(edges):
-            return z_all[:, PACK * edges[0] : PACK * edges[1]]
-
-        def width(edges):
-            return edges[1] - edges[0]
-
-        in_order = range(PACK)
         sums_a = keep.tile([P, PACK, width(EDGES_A)], F32, name="sums_a")
-        edge_values(z_of(EDGES_A), sums_a[:], EDGES_A, last_e)
-        edge_values(z_of(EDGES_B), src_apart.rearrange("p (t n) -> p t n", t=PACK), EDGES_B, in_order)
-        high_halves = src_rest[:].rearrange("p (t n) -> p t n", n=BANK)[:, ::2, :]
-        edge_values(z_of(EDGES_C), high_halves[:, :, : width(EDGES_C)], EDGES_C, in_order)
+        edge_values(sums_a[:], EDGES_A, range(PACK))
+        edge_values(apart[:].rearrange("p (t n) -> p t n", t=PACK), EDGES_B, last_first)
+        edge_values(late[:, :, : width(EDGES_C)], EDGES_C, last_first)
         codes_a, scales_a = quantise_edges(EDGES_A)
         half_a = width(EDGES_A) // 2
-        store(second_product(codes_a[:, :half_a], scales_a[:, :half_a], FIRST_BANKS), 0, nc.scalar.copy)
-        late_a = second_product(codes_a[:, half_a:], scales_a[:, half_a:], 0)
-        edge_values(z_of(EDGES_D), sums_a[:, :, : width(EDGES_D)], EDGES_D, in_order)
-        store(late_a, half_a, nc.vector.tensor_copy)
+        store(second_product(codes_a[:, :half_a], scales_a[:, :half_a], 2), 0, on_scalar)
+        late_a = second_product(codes_a[:, half_a:], scales_a[:, half_a:], 3)
+        edge_values(sums_a[:, :, : width(EDGES_D)], EDGES_D, last_first)
+        store(late_a, half_a, on_vector)
         for n, edges in enumerate([EDGES_B, *LAST_PRODUCTS]):
-            store(second_product(*quantise_edges(edges), FIRST_BANKS + 1 + n), edges[0], nc.scalar.copy)
+            store(second_product(*quantise_edges(edges), 4 + n), edges[0], on_scalar)

@@ -178,7 +178,10 @@ def tile_picked_hub_silu_e_kernel(tc, xT, w1, w2, w3, offs, src, dst, out):
         apart = held.tile([P, 2 * BANK], F32, name="apart", offset=9 * KIB, align_bytes=64)
         stage_w3 = held.tile([P, GROUPED], BF16, name="stage_w3", offset=8 * KIB, align_bytes=64)
         early[3] = apart[:, P : P + BANK]
-        gpsimd_round(stage_w3[:].rearrange("p (n t) -> p n t", t=PACK), w3_raw[:].rearrange("p t n -> p n t"))
+        nc.vector.tensor_copy(
+            stage_w3[:].rearrange("p (c i t) -> p c t i", i=RUN, t=PACK),
+            w3_raw[:].rearrange("p t (c i) -> p c t i", i=RUN),
+        )
         nc.vector.tensor_copy(early[3], rows[0, 3].indirect(entries(src_t, *EDGES_A)))
         nc.vector.tensor_copy(middle_3[:], rows[0, 3].indirect(entries(src_t, *EDGES_B)))
         quantise_weights(["w3"], stage_w3[:])

@@ -26,8 +26,9 @@ RUN = 4
 GROUPED = P * PACK
 
 KIB = 1024
-SCALAR_FROM = 704
-NODE_QUARTERS = [(0, 256), (256, 512), (512, 768), (768, 1024)]
+LAST_QUARTER = 768
+SCALAR_FROM = 640
+NODE_QUARTERS = [(0, 256), (256, 512), (768, 1024), (512, 768)]
 VECTOR_PIECES = [(0, 384), (384, SCALAR_FROM)]
 HALVES = [(0, BANK), (BANK, 2 * BANK)]
 EDGES_A, EDGES_B, EDGES_C, EDGES_D = (0, 512), (512, 768), (768, 928), (928, 1024)
@@ -63,29 +64,35 @@ def tile_picked_hub_silu_e_kernel(tc, xT, w1, w2, w3, offs, src, dst, out):
         nc.sync.dma_start(offs_t[:], offs)
         for j in range(PACK):
             nc.sync.dma_start(raw[j][:], x_rows[j])
-        w_raw = []
-        for name, w, list_tile, list_in in (("w1", w1, src_t, src), ("w2", w2, dst_t, dst)):
-            w_tile = keep.tile([P, PACK * H], F32, name=f"{name}_raw", align_bytes=64)
-            nc.sync.dma_start(w_tile[:], w.rearrange("(p j) c -> p (j c)", j=PACK))
-            nc.sync.dma_start(list_tile[:], list_in)
-            w_raw.append(w_tile[:])
+        front = 2 * LAST_QUARTER - BLOCK_ROWS
+        w1_tile = keep.tile([P, front + PACK * H], F32, name="w1_tile", align_bytes=64)
+        w2_tile = keep.tile([P, PACK * H], F32, name="w2_tile", align_bytes=64)
+        nc.sync.dma_start(w1_tile[:, front:], w1.rearrange("(p j) c -> p (j c)", j=PACK))
+        nc.sync.dma_start(src_t[:], src)
+        nc.sync.dma_start(w2_tile[:], w2.rearrange("(p j) c -> p (j c)", j=PACK))
+        nc.sync.dma_start(dst_t[:], dst)
+        w_raw = [w1_tile[:, front:], w2_tile[:]]
         w3_raw = keep.tile([P, PACK, N], F32, name="w3_raw")
         w3_rows = w3.rearrange("(b t q) n -> t b q n", t=PACK, q=BLOCK_ROWS)
         for t in range(PACK):
             nc.sync.dma_start(w3_raw[:, t, :], w3_rows[t])
 
-        woven = keep.tile([P, S * PACK], BF16, name="woven", align_bytes=64)
-        woven_rows = woven[:].rearrange("p (n j) -> p j n", j=PACK)
+        woven = w1_tile[:, : 2 * LAST_QUARTER].bitcast(BF16)
+        woven_last = keep.tile([P, (S - LAST_QUARTER) * PACK], BF16, name="woven_last", align_bytes=64)
+        woven_rows = woven.rearrange("p (n j) -> p j n", j=PACK)
         planes = keep.tile([P, PACK, S - SCALAR_FROM], BF16, name="planes", align_bytes=64)
         for j in range(PACK):
             nc.scalar.activation(planes[:, j, :], raw[j][:].indirect(entries(offs_t, SCALAR_FROM, S)), COPY)
             for a, b in VECTOR_PIECES if j == PACK - 1 else [(0, SCALAR_FROM)]:
                 nc.vector.tensor_copy(woven_rows[:, j, a:b], raw[j][:].indirect(entries(offs_t, a, b)))
 
-        nc.scalar.copy(
-            woven[:, SCALAR_FROM * PACK :].rearrange("p (c i j) -> p c j i", i=LINE_COLUMNS, j=PACK),
-            planes[:].rearrange("p j (c i) -> p c j i", i=LINE_COLUMNS),
-        )
+        def interleave(target, a, b):
+            nc.scalar.copy(
+                target.rearrange("p (c i j) -> p c j i", i=LINE_COLUMNS, j=PACK),
+                planes[:, :, a - SCALAR_FROM : b - SCALAR_FROM].rearrange("p j (c i) -> p c j i", i=LINE_COLUMNS),
+            )
+
+        interleave(woven_last[:], LAST_QUARTER, S)
 
         weights = {}
 
@@ -116,29 +123,30 @@ def tile_picked_hub_silu_e_kernel(tc, xT, w1, w2, w3, offs, src, dst, out):
             return tile[:, n * GROUPED : (n + 1) * GROUPED]
 
         x_scales = keep.tile([P, S], U8, name="x_scales", align_bytes=64)
-        x_low = keep.tile([P, BANK], U32, name="x_low", align_bytes=64)
-
-        def x_codes(a, b):
-            return x_low[:, a:b] if a < BANK else x_high[:, a - BANK : b - BANK]
+        x_codes = held.tile([P, S], U32, name="x_codes", offset=14 * KIB, align_bytes=64)
 
         def quantise_nodes(a, b):
-            nc.vector.quantize_mx(out=x_codes(a, b).bitcast(FP8X4), scales=x_scales[:, a:b], in_=woven[:, a * PACK : b * PACK])
+            nc.vector.quantize_mx(
+                out=x_codes[:, a:b].bitcast(FP8X4),
+                scales=x_scales[:, a:b],
+                in_=woven_last[:] if b == S else woven[:, a * PACK : b * PACK],
+            )
 
-        for a, b in NODE_QUARTERS[:2]:
+        for a, b in NODE_QUARTERS[:3]:
             quantise_nodes(a, b)
-        first_grouped = held.tile([P, GROUPED], BF16, name="first_grouped", offset=13 * KIB, align_bytes=64)
-        second_grouped = keep.tile([P, GROUPED], BF16, name="second_grouped", align_bytes=64)
-        group_weights(0, 0, nc.vector.tensor_copy, RUN, first_grouped[:])
-        group_weights(0, 1, nc.vector.tensor_copy, RUN, second_grouped[:])
+        first_grouped = held.tile([P, GROUPED], BF16, name="first_grouped", offset=7 * KIB, align_bytes=64)
+        for lo in (0, 8):
+            group_weights(0, 0, nc.scalar.copy, LINE_COLUMNS, first_grouped[:], lo, lo + 8)
         quantise_weights([(0, 0)], first_grouped[:])
-        quantise_weights([(0, 1)], second_grouped[:])
-        x_high = held.tile([P, BANK], U32, name="x_high", offset=13 * KIB, align_bytes=64)
-        for a, b in NODE_QUARTERS[2:]:
-            quantise_nodes(a, b)
-        stage_y = held.tile([P, 2 * GROUPED], BF16, name="stage_y", offset=7 * KIB, align_bytes=64)
-        for n in range(2):
-            group_weights(0, 2 + n, nc.scalar.copy, LINE_COLUMNS, slot(stage_y, n))
-        quantise_weights([(0, 2), (0, 3)], stage_y[:])
+        interleave(woven[:, SCALAR_FROM * PACK :], SCALAR_FROM, LAST_QUARTER)
+        stage_y = held.tile([P, 3 * GROUPED], BF16, name="stage_y", offset=7 * KIB, align_bytes=64)
+        group_weights(0, 1, nc.vector.tensor_copy, RUN, slot(stage_y, 0))
+        quantise_nodes(*NODE_QUARTERS[3])
+        group_weights(0, 2, nc.vector.tensor_copy, RUN, slot(stage_y, 1))
+        quantise_weights([(0, 1)], slot(stage_y, 0))
+        group_weights(0, 3, nc.vector.tensor_copy, RUN, slot(stage_y, 2))
+        quantise_weights([(0, 2)], slot(stage_y, 1))
+        quantise_weights([(0, 3)], slot(stage_y, 2))
 
         rows = {(side, t): keep.tile([P, S], F32, name=f"rows_{side}_{t}")[:] for side in range(2) for t in range(PACK)}
 
@@ -150,7 +158,7 @@ def tile_picked_hub_silu_e_kernel(tc, xT, w1, w2, w3, offs, src, dst, out):
                     out=acc[:, : b - a],
                     lhsT=codes.bitcast(FP8X4),
                     lhsT_scale=scales,
-                    rhs=x_codes(a, b).bitcast(FP8X4),
+                    rhs=x_codes[:, a:b].bitcast(FP8X4),
                     rhs_scale=x_scales[:, a:b],
                     start=True,
                     stop=True,
@@ -158,7 +166,7 @@ def tile_picked_hub_silu_e_kernel(tc, xT, w1, w2, w3, offs, src, dst, out):
                 engine_copy(rows[key][:, a:b], acc[:, : b - a])
 
         on_scalar, on_vector = nc.scalar.copy, nc.vector.tensor_copy
-        first_product((0, 0), NODE_QUARTERS, range(4), [on_scalar, on_scalar, on_scalar, on_vector])
+        first_product((0, 0), NODE_QUARTERS, range(4), [on_scalar] * 4)
 
         early = {t: keep.tile([P, EDGES_B[1] if t == 0 else BANK], F32, name=f"early_{t}")[:] for t in range(3)}
 
@@ -187,7 +195,7 @@ def tile_picked_hub_silu_e_kernel(tc, xT, w1, w2, w3, offs, src, dst, out):
         quantise_weights(["w3"], stage_w3[:])
         for t, banks in enumerate([(2, 3), (4, 5), (6, 7), (0, 1)]):
             first_product((1, t), HALVES, banks, [on_scalar] * 2)
-        late = held.tile([P, PACK, BANK], F32, name="late", offset=13 * KIB, align_bytes=64)
+        late = held.tile([P, PACK, BANK], F32, name="late", offset=14 * KIB, align_bytes=64)
         last_first = (3, 0, 1, 2)
         for t in (1, 2):
             scalar_gather(late[:, t, : width(EDGES_B)], t, *EDGES_B)

@@ -178,21 +178,22 @@ def tile_picked_hub_silu_e_kernel(tc, xT, w1, w2, w3, offs, src, dst, out):
             first_product((0, t), HALVES, banks, [on_vector] * 2)
             if t < 3:
                 scalar_gather(early[t], t, *EDGES_A)
-        stage_e = held.tile([P, PACK * GROUPED], BF16, name="stage_e", offset=7 * KIB, align_bytes=64)
-        for t in range(PACK):
+        stage_e = held.tile([P, 3 * GROUPED], BF16, name="stage_e", offset=7 * KIB, align_bytes=64)
+        for t in range(3):
             group_on_gpsimd(1, t, slot(stage_e, t))
-        quantise_weights([(1, t) for t in range(PACK)], stage_e[:])
-        middle_3 = held.tile([P, width(EDGES_B)], F32, name="middle_3", offset=7 * KIB, align_bytes=64)
+        quantise_weights([(1, t) for t in range(3)], stage_e[:])
+        stage_last = held.tile([P, 2 * GROUPED], BF16, name="stage_last", offset=6 * KIB, align_bytes=64)
+        middle_3 = held.tile([P, width(EDGES_B)], F32, name="middle_3", offset=8 * KIB, align_bytes=64)
         apart = held.tile([P, 2 * BANK], F32, name="apart", offset=9 * KIB, align_bytes=64)
-        stage_w3 = held.tile([P, GROUPED], BF16, name="stage_w3", offset=8 * KIB, align_bytes=64)
         early[3] = apart[:, P : P + BANK]
+        group_weights(1, 3, on_vector, RUN, slot(stage_last, 0))
         nc.vector.tensor_copy(
-            stage_w3[:].rearrange("p (c i t) -> p c t i", i=RUN, t=PACK),
+            slot(stage_last, 1).rearrange("p (c i t) -> p c t i", i=RUN, t=PACK),
             w3_raw[:].rearrange("p t (c i) -> p c t i", i=RUN),
         )
         nc.vector.tensor_copy(early[3], rows[0, 3].indirect(entries(src_t, *EDGES_A)))
+        quantise_weights([(1, 3), "w3"], stage_last[:])
         nc.vector.tensor_copy(middle_3[:], rows[0, 3].indirect(entries(src_t, *EDGES_B)))
-        quantise_weights(["w3"], stage_w3[:])
         for t, banks in enumerate([(2, 3), (4, 5), (6, 7), (0, 1)]):
             first_product((1, t), HALVES, banks, [on_scalar] * 2)
         late = held.tile([P, PACK, BANK], F32, name="late", offset=14 * KIB, align_bytes=64)

@@ -31,7 +31,7 @@ SCALAR_FROM = 640
 NODE_QUARTERS = [(0, 256), (256, 512), (768, 1024), (512, 768)]
 VECTOR_PIECES = [(0, 384), (384, SCALAR_FROM)]
 HALVES = [(0, BANK), (BANK, 2 * BANK)]
-EDGES_A, EDGES_B, EDGES_C, EDGES_D = (0, 512), (512, 768), (768, 928), (928, 1024)
+EDGES_A, EDGES_B, EDGES_C, EDGES_D = (0, 512), (512, 768), (768, 960), (960, 1024)
 LAST_PRODUCTS = [(768, 896), (896, 1024)]
 
 
@@ -199,8 +199,8 @@ def tile_picked_hub_silu_e_kernel(tc, xT, w1, w2, w3, offs, src, dst, out):
         late = held.tile([P, PACK, BANK], F32, name="late", offset=14 * KIB, align_bytes=64)
         last_first = (3, 0, 1, 2)
         for t in (1, 2):
-            scalar_gather(late[:, t, : width(EDGES_B)], t, *EDGES_B)
-        for t in last_first:
+            scalar_gather(late[:, t, :], t, BANK, U)
+        for t in (3, 0):
             scalar_gather(late[:, t, width(EDGES_B) :], t, EDGES_C[0], U)
 
         def from_src(t, a, b):

@@ -26,6 +26,7 @@ RUN = 4
 GROUPED = P * PACK
 
 KIB = 1024
+SHARED_AT = 640
 LAST_QUARTER = 768
 SCALAR_FROM = 640
 NODE_QUARTERS = [(0, 256), (256, 512), (768, 1024), (512, 768)]
@@ -183,31 +184,29 @@ def tile_picked_hub_silu_e_kernel(tc, xT, w1, w2, w3, offs, src, dst, out):
             group_on_gpsimd(1, t, slot(stage_e, t))
         quantise_weights([(1, t) for t in range(3)], stage_e[:])
         stage_last = held.tile([P, 2 * GROUPED], BF16, name="stage_last", offset=6 * KIB, align_bytes=64)
-        middle_3 = held.tile([P, width(EDGES_B)], F32, name="middle_3", offset=8 * KIB, align_bytes=64)
-        apart = held.tile([P, 2 * BANK], F32, name="apart", offset=9 * KIB, align_bytes=64)
+        apart = keep.tile([P, 2 * BANK], F32, name="apart")
         early[3] = apart[:, P : P + BANK]
+        nc.vector.tensor_copy(early[3][:, : BANK // 2], rows[0, 3].indirect(entries(src_t, 0, BANK // 2)))
         group_weights(1, 3, on_vector, RUN, slot(stage_last, 0))
         nc.vector.tensor_copy(
             slot(stage_last, 1).rearrange("p (c i t) -> p c t i", i=RUN, t=PACK),
             w3_raw[:].rearrange("p t (c i) -> p c t i", i=RUN),
         )
-        nc.vector.tensor_copy(early[3], rows[0, 3].indirect(entries(src_t, *EDGES_A)))
+        nc.vector.tensor_copy(early[3][:, BANK // 2 :], rows[0, 3].indirect(entries(src_t, BANK // 2, BANK)))
         quantise_weights([(1, 3), "w3"], stage_last[:])
-        nc.vector.tensor_copy(middle_3[:], rows[0, 3].indirect(entries(src_t, *EDGES_B)))
         for t, banks in enumerate([(2, 3), (4, 5), (6, 7), (0, 1)]):
             first_product((1, t), HALVES, banks, [on_scalar] * 2)
         late = held.tile([P, PACK, BANK], F32, name="late", offset=14 * KIB, align_bytes=64)
         last_first = (3, 0, 1, 2)
+        scalar_gather(late[:, 3, SHARED_AT - BANK :], 3, SHARED_AT, U)
         for t in (1, 2):
             scalar_gather(late[:, t, :], t, BANK, U)
-        for t in (3, 0):
-            scalar_gather(late[:, t, width(EDGES_B) :], t, EDGES_C[0], U)
+        nc.vector.tensor_copy(late[:, 3, : SHARED_AT - BANK], rows[0, 3].indirect(entries(src_t, BANK, SHARED_AT)))
+        scalar_gather(late[:, 0, width(EDGES_B) :], 0, EDGES_C[0], U)
 
         def from_src(t, a, b):
             if b <= early[t].shape[1]:
                 return early[t][:, a:b]
-            if t == 3 and (a, b) == EDGES_B:
-                return middle_3[:]
             return late[:, t, a - BANK : b - BANK]
 
         z_all = keep.tile([P, U * PACK], BF16, name="z_all", align_bytes=64)

from contextlib import ExitStack

import concourse.mybir as mybir

K, T, S, H, N, U = 512, 2048, 1024, 512, 128, 1024
FLOPS = 2 * K * H * S * 2 + 2 * H * N * U

F32 = mybir.dt.float32
BF16 = mybir.dt.bfloat16
U32 = mybir.dt.uint32
U16 = mybir.dt.uint16
U8 = mybir.dt.uint8
FP8X4 = mybir.dt.float8_e4m3fn_x4
ADD = mybir.AluOpType.add
MULT = mybir.AluOpType.mult
COPY = mybir.ActivationFunctionType.Copy
SILU = mybir.ActivationFunctionType.Silu

P = 128
PACK = 4
LIST_ROWS = 16
BANK = 512
BLOCK_ROWS = 8
LINE_COLUMNS = 2
RUN = 4
GROUPED = P * PACK

KIB = 1024
SHARED_AT = 640
LAST_QUARTER = 768
SCALAR_FROM = 640
NODE_QUARTERS = [(0, 256), (256, 512), (768, 1024), (512, 768)]
VECTOR_PIECES = [(0, 384), (384, SCALAR_FROM)]
HALVES = [(0, BANK), (BANK, 2 * BANK)]
EDGES_A, EDGES_B, EDGES_C, EDGES_D = (0, 512), (512, 768), (768, 960), (960, 1024)
LAST_PRODUCTS = [(768, 896), (896, 1024)]


def tile_picked_hub_silu_e_kernel(tc, xT, w1, w2, w3, offs, src, dst, out):
    nc = tc.nc
    with ExitStack() as ctx:
        keep = ctx.enter_context(tc.tile_pool(name="keep", bufs=1))
        held = ctx.enter_context(tc.tile_pool(name="held", bufs=1))
        psum = ctx.enter_context(tc.psum_pool(name="psum", bufs=1))

        def bank(number, name):
            return psum.tile([P, BANK], F32, name=name, tag=f"bank_{number}")

        warm = keep.tile([P, 2], F32, name="warm")
        nc.vector.memset(warm[:, 0:1], 0.0)
        nc.scalar.activation(warm[:, 1:2], warm[:, 0:1], SILU)

        offs_t = keep.tile([P, S // LIST_ROWS], U16, name="offs_t")
        src_t = keep.tile([P, U // LIST_ROWS], U16, name="src_t")
        dst_t = keep.tile([P, U // LIST_ROWS], U16, name="dst_t")

        def width(edges):
            return edges[1] - edges[0]

        def entries(list_tile, a, b):
            return list_tile[:, a // LIST_ROWS : b // LIST_ROWS]

        x_rows = xT.rearrange("(p j) n -> j p n", j=PACK)
        raw = [keep.tile([P, T], F32, name=f"raw_{j}") for j in range(PACK)]
        nc.sync.dma_start(offs_t[:], offs)
        for j in range(PACK):
            nc.sync.dma_start(raw[j][:], x_rows[j])
        front = 2 * LAST_QUARTER - BLOCK_ROWS
        w1_tile = keep.tile([P, front + PACK * H], F32, name="w1_tile", align_bytes=64)
        w2_tile = keep.tile([P, PACK * H], F32, name="w2_tile", align_bytes=64)
        nc.sync.dma_start(w1_tile[:, front:], w1.rearrange("(p j) c -> p (j c)", j=PACK))
        nc.sync.dma_start(src_t[:], src)
        nc.sync.dma_start(w2_tile[:], w2.rearrange("(p j) c -> p (j c)", j=PACK))
        nc.sync.dma_start(dst_t[:], dst)
        w_raw = [w1_tile[:, front:], w2_tile[:]]
        w3_raw = keep.tile([P, PACK, N], F32, name="w3_raw")
        w3_rows = w3.rearrange("(b t q) n -> t b q n", t=PACK, q=BLOCK_ROWS)
        for t in range(PACK):
            nc.sync.dma_start(w3_raw[:, t, :], w3_rows[t])

        woven = w1_tile[:, : 2 * LAST_QUARTER].bitcast(BF16)
        woven_last = keep.tile([P, (S - LAST_QUARTER) * PACK], BF16, name="woven_last", align_bytes=64)
        woven_rows = woven.rearrange("p (n j) -> p j n", j=PACK)
        planes = keep.tile([P, PACK, S - SCALAR_FROM], BF16, name="planes", align_bytes=64)
        for j in range(PACK):
            nc.scalar.activation(planes[:, j, :], raw[j][:].indirect(entries(offs_t, SCALAR_FROM, S)), COPY)
            for a, b in VECTOR_PIECES if j == PACK - 1 else [(0, SCALAR_FROM)]:
                nc.vector.tensor_copy(woven_rows[:, j, a:b], raw[j][:].indirect(entries(offs_t, a, b)))

        def interleave(target, a, b):
            nc.scalar.copy(
                target.rearrange("p (c i j) -> p c j i", i=LINE_COLUMNS, j=PACK),
                planes[:, :, a - SCALAR_FROM : b - SCALAR_FROM].rearrange("p j (c i) -> p c j i", i=LINE_COLUMNS),
            )

        interleave(woven_last[:], LAST_QUARTER, S)

        weights = {}

        def group_weights(side, t, engine_copy, run, grouped, lo=0, hi=P // BLOCK_ROWS):
            engine_copy(
                grouped.rearrange("p (b g i j) -> p b g j i", g=BLOCK_ROWS // run, i=run, j=PACK)[:, lo:hi],
                w_raw[side].rearrange("p (j b t g i) -> p t b g j i", j=PACK, t=PACK, g=BLOCK_ROWS // run, i=run)[:, t, lo:hi],
            )

        def gpsimd_round(target, source):
            nc.gpsimd.tensor_scalar(target, source, 1.0, 0.0, MULT, ADD)

        def group_on_gpsimd(side, t, grouped):
            gpsimd_round(
                grouped.rearrange("p (b q j) -> p b q j", q=BLOCK_ROWS, j=PACK),
                w_raw[side].rearrange("p (j b t q) -> p t b q j", j=PACK, t=PACK, q=BLOCK_ROWS)[:, t],
            )

        def quantise_weights(keys, grouped):
            name = f"{keys[0][0]}_{keys[0][1]}"
            codes = keep.tile([P, len(keys) * P], U32, name=f"wc_{name}", align_bytes=64)
            scales = keep.tile([P, len(keys) * P], U8, name=f"ws_{name}", align_bytes=64)
            nc.vector.quantize_mx(out=codes[:].bitcast(FP8X4), scales=scales[:], in_=grouped)
            for n, key in enumerate(keys):
                weights[key] = (codes[:, n * P : (n + 1) * P], scales[:, n * P : (n + 1) * P])

        def slot(tile, n):
            return tile[:, n * GROUPED : (n + 1) * GROUPED]

        x_scales = keep.tile([P, S], U8, name="x_scales", align_bytes=64)
        x_codes = held.tile([P, S], U32, name="x_codes", offset=14 * KIB, align_bytes=64)

        def quantise_nodes(a, b):
            nc.vector.quantize_mx(
                out=x_codes[:, a:b].bitcast(FP8X4),
                scales=x_scales[:, a:b],
                in_=woven_last[:] if b == S else woven[:, a * PACK : b * PACK],
            )

        for a, b in NODE_QUARTERS[:3]:
            quantise_nodes(a, b)
        first_grouped = held.tile([P, GROUPED], BF16, name="first_grouped", offset=7 * KIB, align_bytes=64)
        for lo in (0, 8):
            group_weights(0, 0, nc.scalar.copy, LINE_COLUMNS, first_grouped[:], lo, lo + 8)
        quantise_weights([(0, 0)], first_grouped[:])
        interleave(woven[:, SCALAR_FROM * PACK :], SCALAR_FROM, LAST_QUARTER)
        stage_y = held.tile([P, 3 * GROUPED], BF16, name="stage_y", offset=7 * KIB, align_bytes=64)
        group_weights(0, 1, nc.vector.tensor_copy, RUN, slot(stage_y, 0))
        quantise_nodes(*NODE_QUARTERS[3])
        group_weights(0, 2, nc.vector.tensor_copy, RUN, slot(stage_y, 1))
        quantise_weights([(0, 1)], slot(stage_y, 0))
        group_weights(0, 3, nc.vector.tensor_copy, RUN, slot(stage_y, 2))
        quantise_weights([(0, 2)], slot(stage_y, 1))
        quantise_weights([(0, 3)], slot(stage_y, 2))

        rows = {(side, t): keep.tile([P, S], F32, name=f"rows_{side}_{t}")[:] for side in range(2) for t in range(PACK)}

        def first_product(key, cuts, banks, copies):
            codes, scales = weights[key]
            for (a, b), number, engine_copy in zip(cuts, banks, copies):
                acc = bank(number, "acc")
                nc.tensor.matmul_mx(
                    out=acc[:, : b - a],
                    lhsT=codes.bitcast(FP8X4),
                    lhsT_scale=scales,
                    rhs=x_codes[:, a:b].bitcast(FP8X4),
                    rhs_scale=x_scales[:, a:b],
                    start=True,
                    stop=True,
                )
                engine_copy(rows[key][:, a:b], acc[:, : b - a])

        on_scalar, on_vector = nc.scalar.copy, nc.vector.tensor_copy
        first_product((0, 0), NODE_QUARTERS, range(4), [on_scalar] * 4)

        early = {t: keep.tile([P, EDGES_B[1] if t == 0 else BANK], F32, name=f"early_{t}")[:] for t in range(3)}

        def scalar_gather(target, t, a, b):
            nc.scalar.activation(target, rows[0, t].indirect(entries(src_t, a, b)), COPY)

        scalar_gather(early[0], 0, 0, EDGES_B[1])
        for t, banks in ((1, (4, 5)), (2, (6, 7)), (3, (0, 1))):
            first_product((0, t), HALVES, banks, [on_vector] * 2)
            if t < 3:
                scalar_gather(early[t], t, *EDGES_A)
        stage_e = held.tile([P, 3 * GROUPED], BF16, name="stage_e", offset=7 * KIB, align_bytes=64)
        for t in range(3):
            group_on_gpsimd(1, t, slot(stage_e, t))
        quantise_weights([(1, t) for t in range(3)], stage_e[:])
        stage_last = held.tile([P, 2 * GROUPED], BF16, name="stage_last", offset=6 * KIB, align_bytes=64)
        apart = keep.tile([P, 2 * BANK], F32, name="apart")
        early[3] = apart[:, P : P + BANK]
        nc.vector.tensor_copy(early[3][:, : BANK // 2], rows[0, 3].indirect(entries(src_t, 0, BANK // 2)))
        group_weights(1, 3, on_vector, RUN, slot(stage_last, 0))
        nc.vector.tensor_copy(
            slot(stage_last, 1).rearrange("p (c i t) -> p c t i", i=RUN, t=PACK),
            w3_raw[:].rearrange("p t (c i) -> p c t i", i=RUN),
        )
        nc.vector.tensor_copy(early[3][:, BANK // 2 :], rows[0, 3].indirect(entries(src_t, BANK // 2, BANK)))
        quantise_weights([(1, 3), "w3"], stage_last[:])
        for t, banks in enumerate([(2, 3), (4, 5), (6, 7), (0, 1)]):
            first_product((1, t), HALVES, banks, [on_scalar] * 2)
        late = held.tile([P, PACK, BANK], F32, name="late", offset=14 * KIB, align_bytes=64)
        last_first = (3, 0, 1, 2)
        scalar_gather(late[:, 3, SHARED_AT - BANK :], 3, SHARED_AT, U)
        for t in (1, 2):
            scalar_gather(late[:, t, :], t, BANK, U)
        nc.vector.tensor_copy(late[:, 3, : SHARED_AT - BANK], rows[0, 3].indirect(entries(src_t, BANK, SHARED_AT)))
        scalar_gather(late[:, 0, width(EDGES_B) :], 0, EDGES_C[0], U)

        def from_src(t, a, b):
            if b <= early[t].shape[1]:
                return early[t][:, a:b]
            return late[:, t, a - BANK : b - BANK]

        z_all = keep.tile([P, U * PACK], BF16, name="z_all", align_bytes=64)

        def z_of(edges):
            return z_all[:, PACK * edges[0] : PACK * edges[1]]

        def quantise_edges(edges):
            a, b = edges
            z_codes = keep.tile([P, b - a], U32, name=f"zc_{a}", align_bytes=64)
            z_scales = keep.tile([P, b - a], U8, name=f"zs_{a}", align_bytes=64)
            nc.vector.quantize_mx(out=z_codes[:].bitcast(FP8X4), scales=z_scales[:], in_=z_of(edges))
            return z_codes[:], z_scales[:]

        def second_product(z_codes, z_scales, number):
            acc = bank(number, "acc_out")[:, : z_codes.shape[1]]
            nc.tensor.matmul_mx(
                out=acc,
                lhsT=weights["w3"][0].bitcast(FP8X4),
                lhsT_scale=weights["w3"][1],
                rhs=z_codes.bitcast(FP8X4),
                rhs_scale=z_scales,
                start=True,
                stop=True,
            )
            return acc

        def store(acc, first, engine_copy):
            last = first + acc.shape[1]
            done = keep.tile([P, last - first], F32, name=f"done_{first}")
            engine_copy(done[:], acc)
            nc.sync.dma_start(out[:, first:last], done[:])

        def edge_values(sums, edges, tiles):
            a, b = edges
            for t in tiles:
                nc.vector.tensor_tensor(sums[:, t, :], rows[1, t].indirect(entries(dst_t, a, b)), from_src(t, a, b), ADD)
            nc.scalar.activation(
                z_of(edges).rearrange("p (c i t) -> p c t i", i=LINE_COLUMNS, t=PACK),
                sums.rearrange("p t (c i) -> p c t i", i=LINE_COLUMNS),
                SILU,
            )

        sums_a = keep.tile([P, PACK, width(EDGES_A)], F32, name="sums_a")
        edge_values(sums_a[:], EDGES_A, range(PACK))
        edge_values(apart[:].rearrange("p (t n) -> p t n", t=PACK), EDGES_B, last_first)
        edge_values(late[:, :, : width(EDGES_C)], EDGES_C, last_first)
        codes_a, scales_a = quantise_edges(EDGES_A)
        half_a = width(EDGES_A) // 2
        store(second_product(codes_a[:, :half_a], scales_a[:, :half_a], 2), 0, on_scalar)
        late_a = second_product(codes_a[:, half_a:], scales_a[:, half_a:], 3)
        edge_values(sums_a[:, :, : width(EDGES_D)], EDGES_D, last_first)
        store(late_a, half_a, on_vector)
        for n, edges in enumerate([EDGES_B, *LAST_PRODUCTS]):
            store(second_product(*quantise_edges(edges), 4 + n), edges[0], on_scalar)
